import numpy as np
import ml_dtypes


def mxq(x, axis, fmt="e4m3"):
    dtype, down = {"e4m3": (ml_dtypes.float8_e4m3fn, 7), "e5m2": (ml_dtypes.float8_e5m2, 14)}[fmt]
    v = np.moveaxis(np.asarray(x, np.float32).astype(ml_dtypes.bfloat16).astype(np.float64), axis, -1)
    blocks = v.reshape(v.shape[:-1] + (-1, 32))
    amax = np.abs(blocks).max(-1, keepdims=True)
    byte = np.maximum(np.where(amax > 0, np.frexp(amax)[1] - 1 + 127, 0) - down, 1)
    scale = np.exp2(byte - 127.0)
    codes = (blocks / scale).astype(np.float32).astype(dtype).astype(np.float64)
    return np.moveaxis((codes * scale).reshape(v.shape), -1, axis)


WIDE = False


def mx_kscale(k):
    if not WIDE:
        return np.ones(k)
    levels = np.array([24, -24, 12, -12, 0])
    if k % 512:
        return np.exp2(np.random.permutation(np.resize(levels, k // 32))).repeat(32)
    a = np.empty((k // 512, 16))
    for p in range(k // 512):
        a[p, :8] = np.random.permutation(np.resize(levels, 8))
        for g in range(8):
            far = levels[np.abs(levels - a[p, g]) >= 10]
            a[p, g + 8] = far[np.random.randint(len(far))]
    return np.exp2(a.ravel()).repeat(32)


def f64(x):
    return np.asarray(x).astype(np.float64)


def striped(idx):
    return np.tile(idx.reshape(-1, 16).T, (8, 1)).astype(np.uint16)


def unstriped(offs):
    return offs[:16].T.reshape(-1).astype(np.int64)


E2M1 = np.array([0.0, 0.5, 1.0, 1.5, 2.0, 3.0, 4.0, 6.0, -0.0, -0.5, -1.0, -1.5, -2.0, -3.0, -4.0, -6.0])


def pack_weight(w, fmt):
    k, n = w.shape
    w = f64(np.asarray(w, np.float32).astype(ml_dtypes.bfloat16)).reshape(k // 32, 32, n)
    amax = np.abs(w).max(1)
    if fmt == "e4m3":
        byte = np.frexp(amax)[1] - 1 + 127 - 7
    else:
        mant, ex = np.frexp(amax / 6.0)
        byte = np.where(mant > 0.5, ex, ex - 1) + 127
    byte = np.clip(np.where(amax > 0, byte, 1), 1, 254)
    scaled = (w * np.exp2(127.0 - byte)[:, None, :]).reshape(k, n).astype(np.float32)
    by_word = np.ascontiguousarray(scaled.reshape(k // 512, 128, 4, n).transpose(0, 1, 3, 2))
    if fmt == "e4m3":
        words = by_word.astype(ml_dtypes.float8_e4m3fn).view(np.uint8)
    else:
        c = by_word.astype(ml_dtypes.float4_e2m1fn).view(np.uint8) & 0xF
        words = (c[..., 0::2] | (c[..., 1::2] << 4)).reshape(k // 512, 128, 2 * n)
    return np.ascontiguousarray(words), np.ascontiguousarray(byte.astype(np.uint8).reshape(k // 512, 16, n))


def unpack_weight(words, scales, fmt):
    g, _, n = scales.shape
    words = np.ascontiguousarray(words).reshape(g, 128, n, -1)
    if fmt == "e4m3":
        vals = words.view(ml_dtypes.float8_e4m3fn).astype(np.float64)
    else:
        nib = np.empty((g, 128, n, 4), np.uint8)
        nib[..., 0::2] = words & 0xF
        nib[..., 1::2] = words >> 4
        vals = E2M1[nib]
    vals = vals * np.repeat(np.exp2(scales.astype(np.float64) - 127.0), 8, axis=1)[..., None]
    return vals.transpose(0, 1, 3, 2).reshape(g * 512, n)


def sigm(f):
    return 1.0 / (1.0 + np.exp(-np.maximum(f, -700.0)))


K, N, T, J = 512, 512, 2048, 1024


def setup_inputs():
    n = np.random.standard_normal
    s = mx_kscale(K)[:, None]
    p_tab = pack_weight(n((K, T)) * s, "e4m3")
    p_wb = pack_weight(n((K, N)) / np.sqrt(2 * K) / s, "e2m1")
    p_wc = pack_weight(n((K, N)) / np.sqrt(K) / s, "e4m3")
    return {
        "tab_words": p_tab[0],
        "tab_scales": p_tab[1],
        "wa": (n((K, N)) / np.sqrt(2 * K) / s).astype(np.float32),
        "wb_words": p_wb[0],
        "wb_scales": p_wb[1],
        "wc_words": p_wc[0],
        "wc_scales": p_wc[1],
        "wo": (n((K, N)) / np.sqrt(K) / s).astype(np.float32),
        "rT": (n((N, T))).astype(np.float32),
        "wgo": np.tile(np.random.uniform(0.5, 2.0, J), (128, 1)).astype(np.float32),
        "offs": striped(np.random.permutation(T)[:J]),
        "offs2": striped(np.random.permutation(T)[:J]),
    }


def reference(tab_words, tab_scales, wa, wb_words, wb_scales, wc_words, wc_scales, wo, rT, wgo, offs, offs2):
    idx = unstriped(offs)
    idx2 = unstriped(offs2)
    tab_ = unpack_weight(tab_words, tab_scales, "e4m3")[:, idx]
    tabb_ = unpack_weight(tab_words, tab_scales, "e4m3")[:, idx2]
    wa_ = mxq(f64(wa), 0, "e4m3")
    wb_ = unpack_weight(wb_words, wb_scales, "e2m1")
    za = wa_.T @ tabb_ + wb_.T @ tab_
    eta = sigm(za)
    wc_ = unpack_weight(wc_words, wc_scales, "e4m3")
    ms = wc_.T @ tab_
    wo_ = mxq(f64(wo), 0, "e4m3")
    ow = wo_.T @ tabb_
    out = np.zeros((N, T))
    out[:, idx2] = f64(wgo)[0] * (ow + eta * ms + f64(rT)[:, idx2])
    return out

@@ -1,0 +1,187 @@
+from contextlib import ExitStack
+
+import concourse.mybir as mybir
+from concourse.masks import make_identity
+
+K, N, T, J = 512, 512, 2048, 1024
+FLOPS = 4 * 2 * K * N * J
+
+F32 = mybir.dt.float32
+BF16 = mybir.dt.bfloat16
+I32 = mybir.dt.int32
+U32 = mybir.dt.uint32
+U16 = mybir.dt.uint16
+U8 = mybir.dt.uint8
+FP8X4 = mybir.dt.float8_e4m3fn_x4
+FP4X4 = mybir.dt.float4_e2m1fn_x4
+MULT = mybir.AluOpType.mult
+COPY = mybir.ActivationFunctionType.Copy
+SIGMOID = mybir.ActivationFunctionType.Sigmoid
+
+P = 128
+PACK = 4
+BANK = 512
+EDGE_TILES = J // P
+ROW_BLOCKS = N // P
+HALVES = J // BANK
+TILES_PER_HALF = BANK // P
+LIST_COLS_PER_HALF = BANK // 16
+
+
+def load_scale_rows(nc, plane, scales):
+    rows = scales[0].bitcast(I32)
+    for q in range(4):
+        nc.sync.dma_start(out=plane[32 * q : 32 * q + 4, :], in_=rows[4 * q : 4 * q + 4, :])
+
+
+def tile_list_rgg_ownL_kernel(
+    tc, tab_words, tab_scales, wa, wb_words, wb_scales, wc_words, wc_scales, wo, rT, wgo, offs, offs2, out
+):
+    nc = tc.nc
+    with ExitStack() as ctx:
+        keep = ctx.enter_context(tc.tile_pool(name="keep", bufs=1))
+        ring = ctx.enter_context(tc.tile_pool(name="ring", bufs=3))
+        psum = ctx.enter_context(tc.psum_pool(name="psum", bufs=8))
+
+        src_list = keep.tile([P, J // 16], U16, name="src_list")
+        dst_list = keep.tile([P, J // 16], U16, name="dst_list")
+        tab_w = keep.tile([P, T], I32, name="tab_w", align_bytes=64)
+        tab_s = keep.tile([P, T // 4], I32, name="tab_s", align_bytes=64)
+        wb_w = keep.tile([P, N // 2], I32, name="wb_w", align_bytes=64)
+        wb_s = keep.tile([P, N // 4], I32, name="wb_s", align_bytes=64)
+        wc_w = keep.tile([P, N], I32, name="wc_w", align_bytes=64)
+        wc_s = keep.tile([P, N // 4], I32, name="wc_s", align_bytes=64)
+        wa_raw = keep.tile([P, PACK, N], F32, name="wa_raw")
+        wo_raw = keep.tile([P, PACK, N], F32, name="wo_raw")
+        wgo_rows = keep.tile([P, P], F32, name="wgo_rows")
+        wgo_cols = keep.tile([P, EDGE_TILES], F32, name="wgo_cols")
+        ident = keep.tile([P, P], F32, name="ident")
+        r_rows = [keep.tile([P, T], F32, name=f"r_rows{b}") for b in range(ROW_BLOCKS)]
+        out_rows = [keep.tile([P, T], F32, name=f"out_rows{i}") for i in range(2)]
+
+        nc.vector.memset(tab_s[:], 0)
+        nc.sync.dma_start(dst_list[:], offs2)
+        load_scale_rows(nc, tab_s, tab_scales)
+        nc.sync.dma_start(src_list[:], offs)
+        nc.sync.dma_start(out=tab_w[:], in_=tab_words[0].rearrange("p t i -> p (t i)").bitcast(I32))
+        nc.sync.dma_start(out=wa_raw[:], in_=wa.rearrange("(p i) n -> p i n", i=PACK))
+        nc.vector.memset(wb_s[:], 0)
+        nc.vector.memset(wc_s[:], 0)
+        nc.vector.memset(wgo_rows[:], 0.0)
+        for tile in out_rows:
+            nc.vector.memset(tile[:], 0.0)
+        make_identity(nc, ident[:])
+        nc.sync.dma_start(out=wo_raw[:], in_=wo.rearrange("(p i) n -> p i n", i=PACK))
+        load_scale_rows(nc, wb_s, wb_scales)
+        load_scale_rows(nc, wc_s, wc_scales)
+        nc.sync.dma_start(out=wgo_rows[0:EDGE_TILES, :], in_=wgo[0].rearrange("(e p) -> e p", p=P))
+        nc.sync.dma_start(out=wb_w[:], in_=wb_words[0].bitcast(I32))
+        nc.sync.dma_start(out=wc_w[:], in_=wc_words[0].rearrange("p n i -> p (n i)").bitcast(I32))
+        for b in range(ROW_BLOCKS):
+            nc.sync.dma_start(out=r_rows[b][:], in_=rT[b * P : (b + 1) * P, :])
+
+        src_w = keep.tile([P, J], U32, name="src_w", align_bytes=64)
+        src_s = keep.tile([P, J], U8, name="src_s", align_bytes=64)
+        dst_w = keep.tile([P, J], U32, name="dst_w", align_bytes=64)
+        dst_s = keep.tile([P, J], U8, name="dst_s", align_bytes=64)
+        nc.vector.tensor_copy(dst_s[:], tab_s[:].bitcast(U8).indirect(dst_list[:]))
+        nc.vector.tensor_copy(src_s[:], tab_s[:].bitcast(U8).indirect(src_list[:]))
+        nc.vector.tensor_copy(dst_w[:], tab_w[:].bitcast(U32).indirect(dst_list[:]))
+        nc.vector.tensor_copy(src_w[:], tab_w[:].bitcast(U32).indirect(src_list[:]))
+
+        quantised = []
+        for label, raw in (("wa", wa_raw), ("wo", wo_raw)):
+            grouped = keep.tile([P, N, PACK], BF16, name=f"{label}_grouped", align_bytes=64)
+            codes = keep.tile([P, N], U32, name=f"{label}_codes", align_bytes=64)
+            plane = keep.tile([P, N], U8, name=f"{label}_plane", align_bytes=64)
+            nc.scalar.copy(out=grouped[:], in_=raw[:].rearrange("p i n -> p n i"))
+            nc.vector.quantize_mx(
+                out=codes[:].bitcast(FP8X4), scales=plane[:], in_=grouped[:].rearrange("p n i -> p (n i)")
+            )
+            quantised.append((codes[:].bitcast(FP8X4), plane[:]))
+        wa_mx, wo_mx = quantised
+        wb_mx = (wb_w[:].bitcast(U8).bitcast(FP4X4), wb_s[:].bitcast(U8))
+        wc_mx = (wc_w[:].bitcast(FP8X4), wc_s[:].bitcast(U8))
+
+        wgo_bank = psum.tile([P, BANK], F32, name="bank")
+        nc.tensor.transpose(wgo_bank[:, 0:P], wgo_rows[:], ident[:])
+        nc.scalar.copy(out=wgo_cols[:], in_=wgo_bank[:, 0:EDGE_TILES])
+
+        message = [keep.tile([P, N], F32, name=f"message{e}") for e in range(EDGE_TILES)]
+        own = [keep.tile([P, N], F32, name=f"own{e}") for e in range(EDGE_TILES)]
+        picked = [keep.tile([P, J], F32, name=f"picked{b}") for b in range(ROW_BLOCKS)]
+
+        def mx_pass(bank, words, plane, e, weight, start, stop):
+            cols = slice(e * P, (e + 1) * P)
+            nc.tensor.matmul_mx(
+                out=bank[:],
+                lhsT=words[:, cols].bitcast(FP8X4),
+                lhsT_scale=plane[:, cols],
+                rhs=weight[0],
+                rhs_scale=weight[1],
+                start=start,
+                stop=stop,
+            )
+
+        def edge_tile(e):
+            za = psum.tile([P, BANK], F32, name="bank")
+            mx_pass(za, dst_w, dst_s, e, wa_mx, True, False)
+            mx_pass(za, src_w, src_s, e, wb_mx, False, True)
+            ms = psum.tile([P, BANK], F32, name="bank")
+            mx_pass(ms, src_w, src_s, e, wc_mx, True, True)
+            ow = psum.tile([P, BANK], F32, name="bank")
+            mx_pass(ow, dst_w, dst_s, e, wo_mx, True, True)
+            eta = ring.tile([P, N], F32, name="eta")
+            nc.scalar.activation(eta[:], za[:], SIGMOID)
+            nc.vector.scalar_tensor_tensor(message[e][:], ms[:], wgo_cols[:, e : e + 1], eta[:], MULT, MULT)
+            nc.scalar.activation(own[e][:], ow[:], COPY, scale=wgo_cols[:, e : e + 1])
+
+        def gather_state(b):
+            nc.vector.tensor_copy(picked[b][:], r_rows[b][:].indirect(dst_list[:]))
+
+        def finish(b, h):
+            rows = slice(b * P, (b + 1) * P)
+            turned = psum.tile([P, BANK], F32, name="bank")
+            state = ring.tile([P, BANK], F32, name="state")
+            for q in range(TILES_PER_HALF):
+                e = h * TILES_PER_HALF + q
+                nc.tensor.transpose(turned[:, q * P : (q + 1) * P], picked[b][:, e * P : (e + 1) * P], ident[:])
+            for q in range(TILES_PER_HALF):
+                e = h * TILES_PER_HALF + q
+                cols = slice(q * P, (q + 1) * P)
+                nc.scalar.activation(state[:, cols], turned[:, cols], COPY, scale=wgo_cols[:, e : e + 1])
+            total = psum.tile([P, BANK], F32, name="bank")
+            for q in range(TILES_PER_HALF):
+                e = h * TILES_PER_HALF + q
+                cols = slice(q * P, (q + 1) * P)
+                terms = (own[e][:, rows], message[e][:, rows], state[:, cols])
+                for i, term in enumerate(terms):
+                    nc.tensor.matmul(
+                        total[:, cols], term, ident[:], start=(i == 0), stop=(i == len(terms) - 1), is_transpose=True
+                    )
+            result = ring.tile([P, BANK], F32, name="result")
+            nc.scalar.copy(out=result[:], in_=total[:])
+            offsets = dst_list[:, h * LIST_COLS_PER_HALF : (h + 1) * LIST_COLS_PER_HALF]
+            nc.vector.tensor_copy(out_rows[b % 2][:].indirect(offsets), result[:])
+
+        def store(b):
+            nc.sync.dma_start(out=out[b * P : (b + 1) * P, :], in_=out_rows[b % 2][:])
+
+        gather_state(0)
+        for e in range(TILES_PER_HALF):
+            edge_tile(e)
+        gather_state(1)
+        for e in range(TILES_PER_HALF, EDGE_TILES):
+            edge_tile(e)
+        finish(0, 0)
+        finish(0, 1)
+        store(0)
+        gather_state(2)
+        finish(1, 0)
+        finish(1, 1)
+        store(1)
+        gather_state(3)
+        for b in (2, 3):
+            finish(b, 0)
+            finish(b, 1)
+            store(b)

@@ -26,12 +26,12 @@ ROW_BLOCKS = N // P
 HALVES = J // BANK
 TILES_PER_HALF = BANK // P
 LIST_COLS_PER_HALF = BANK // 16
+OUT_TILES = 3
 
 
-def load_scale_rows(nc, plane, scales):
+def load_scale_quadrant(nc, plane, scales, q):
     rows = scales[0].bitcast(I32)
-    for q in range(4):
-        nc.sync.dma_start(out=plane[32 * q : 32 * q + 4, :], in_=rows[4 * q : 4 * q + 4, :])
+    nc.sync.dma_start(out=plane[32 * q : 32 * (q + 1), :], in_=rows[4 * q : 4 * q + 4, :].partition_broadcast(8))
 
 
 def tile_list_rgg_ownL_kernel(
@@ -57,26 +57,30 @@ def tile_list_rgg_ownL_kernel(
         wgo_cols = keep.tile([P, EDGE_TILES], F32, name="wgo_cols")
         ident = keep.tile([P, P], F32, name="ident")
         r_rows = [keep.tile([P, T], F32, name=f"r_rows{b}") for b in range(ROW_BLOCKS)]
-        out_rows = [keep.tile([P, T], F32, name=f"out_rows{i}") for i in range(2)]
+        out_rows = [keep.tile([P, T], F32, name=f"out_rows{i}") for i in range(OUT_TILES)]
 
-        nc.vector.memset(tab_s[:], 0)
+        make_identity(nc, ident[:])
+        nc.gpsimd.memset(wgo_rows[:], 0.0)
+        warm = keep.tile([P, 1], F32, name="warm")
+        nc.scalar.activation(warm[:], ident[:, 0:1], SIGMOID)
+        for tile in out_rows:
+            nc.gpsimd.memset(tile[:], 0.0)
         nc.sync.dma_start(dst_list[:], offs2)
-        load_scale_rows(nc, tab_s, tab_scales)
+        for q in range(4):
+            load_scale_quadrant(nc, tab_s, tab_scales, q)
         nc.sync.dma_start(src_list[:], offs)
+        load_scale_quadrant(nc, wb_s, wb_scales, 0)
         nc.sync.dma_start(out=tab_w[:], in_=tab_words[0].rearrange("p t i -> p (t i)").bitcast(I32))
         nc.sync.dma_start(out=wa_raw[:], in_=wa.rearrange("(p i) n -> p i n", i=PACK))
-        nc.vector.memset(wb_s[:], 0)
-        nc.vector.memset(wc_s[:], 0)
-        nc.vector.memset(wgo_rows[:], 0.0)
-        for tile in out_rows:
-            nc.vector.memset(tile[:], 0.0)
-        make_identity(nc, ident[:])
+        for q in range(1, 4):
+            load_scale_quadrant(nc, wb_s, wb_scales, q)
+        for q in range(3):
+            load_scale_quadrant(nc, wc_s, wc_scales, q)
         nc.sync.dma_start(out=wo_raw[:], in_=wo.rearrange("(p i) n -> p i n", i=PACK))
-        load_scale_rows(nc, wb_s, wb_scales)
-        load_scale_rows(nc, wc_s, wc_scales)
-        nc.sync.dma_start(out=wgo_rows[0:EDGE_TILES, :], in_=wgo[0].rearrange("(e p) -> e p", p=P))
+        load_scale_quadrant(nc, wc_s, wc_scales, 3)
         nc.sync.dma_start(out=wb_w[:], in_=wb_words[0].bitcast(I32))
         nc.sync.dma_start(out=wc_w[:], in_=wc_words[0].rearrange("p n i -> p (n i)").bitcast(I32))
+        nc.sync.dma_start(out=wgo_rows[0:EDGE_TILES, :], in_=wgo[0].rearrange("(e p) -> e p", p=P))
         for b in range(ROW_BLOCKS):
             nc.sync.dma_start(out=r_rows[b][:], in_=rT[b * P : (b + 1) * P, :])
 
@@ -86,11 +90,15 @@ def tile_list_rgg_ownL_kernel(
         dst_s = keep.tile([P, J], U8, name="dst_s", align_bytes=64)
         nc.vector.tensor_copy(dst_s[:], tab_s[:].bitcast(U8).indirect(dst_list[:]))
         nc.vector.tensor_copy(src_s[:], tab_s[:].bitcast(U8).indirect(src_list[:]))
-        nc.vector.tensor_copy(dst_w[:], tab_w[:].bitcast(U32).indirect(dst_list[:]))
-        nc.vector.tensor_copy(src_w[:], tab_w[:].bitcast(U32).indirect(src_list[:]))
+
+        def half_list(lst, h):
+            return lst[:, h * LIST_COLS_PER_HALF : (h + 1) * LIST_COLS_PER_HALF]
 
         quantised = []
-        for label, raw in (("wa", wa_raw), ("wo", wo_raw)):
+        for h, (label, raw) in enumerate((("wa", wa_raw), ("wo", wo_raw))):
+            cols = slice(h * BANK, (h + 1) * BANK)
+            nc.vector.tensor_copy(dst_w[:, cols], tab_w[:].bitcast(U32).indirect(half_list(dst_list, h)))
+            nc.vector.tensor_copy(src_w[:, cols], tab_w[:].bitcast(U32).indirect(half_list(src_list, h)))
             grouped = keep.tile([P, N, PACK], BF16, name=f"{label}_grouped", align_bytes=64)
             codes = keep.tile([P, N], U32, name=f"{label}_codes", align_bytes=64)
             plane = keep.tile([P, N], U8, name=f"{label}_plane", align_bytes=64)
@@ -133,7 +141,9 @@ def tile_list_rgg_ownL_kernel(
             mx_pass(ow, dst_w, dst_s, e, wo_mx, True, True)
             eta = ring.tile([P, N], F32, name="eta")
             nc.scalar.activation(eta[:], za[:], SIGMOID)
-            nc.vector.scalar_tensor_tensor(message[e][:], ms[:], wgo_cols[:, e : e + 1], eta[:], MULT, MULT)
+            weighted = ring.tile([P, N], F32, name="weighted")
+            nc.scalar.activation(weighted[:], ms[:], COPY, scale=wgo_cols[:, e : e + 1])
+            nc.gpsimd.tensor_tensor(message[e][:], weighted[:], eta[:], MULT)
             nc.scalar.activation(own[e][:], ow[:], COPY, scale=wgo_cols[:, e : e + 1])
 
         def gather_state(b):
@@ -162,26 +172,25 @@ def tile_list_rgg_ownL_kernel(
             result = ring.tile([P, BANK], F32, name="result")
             nc.scalar.copy(out=result[:], in_=total[:])
             offsets = dst_list[:, h * LIST_COLS_PER_HALF : (h + 1) * LIST_COLS_PER_HALF]
-            nc.vector.tensor_copy(out_rows[b % 2][:].indirect(offsets), result[:])
+            nc.vector.tensor_copy(out_rows[b % OUT_TILES][:].indirect(offsets), result[:])
 
         def store(b):
-            nc.sync.dma_start(out=out[b * P : (b + 1) * P, :], in_=out_rows[b % 2][:])
+            nc.sync.dma_start(out=out[b * P : (b + 1) * P, :], in_=out_rows[b % OUT_TILES][:])
 
         gather_state(0)
         for e in range(TILES_PER_HALF):
             edge_tile(e)
         gather_state(1)
-        for e in range(TILES_PER_HALF, EDGE_TILES):
-            edge_tile(e)
         finish(0, 0)
-        finish(0, 1)
-        store(0)
         gather_state(2)
         finish(1, 0)
-        finish(1, 1)
-        store(1)
         gather_state(3)
-        for b in (2, 3):
-            finish(b, 0)
+        for e in range(TILES_PER_HALF, EDGE_TILES):
+            edge_tile(e)
+        finish(2, 0)
+        for b in range(OUT_TILES):
             finish(b, 1)
             store(b)
+        finish(3, 0)
+        finish(3, 1)
+        store(3)

@@ -26,7 +26,7 @@ ROW_BLOCKS = N // P
 HALVES = J // BANK
 TILES_PER_HALF = BANK // P
 LIST_COLS_PER_HALF = BANK // 16
-OUT_TILES = 3
+OUT_TILES = 4
 
 
 def load_scale_quadrant(nc, plane, scales, q):
@@ -41,6 +41,7 @@ def tile_list_rgg_ownL_kernel(
     with ExitStack() as ctx:
         keep = ctx.enter_context(tc.tile_pool(name="keep", bufs=1))
         ring = ctx.enter_context(tc.tile_pool(name="ring", bufs=3))
+        results = ctx.enter_context(tc.tile_pool(name="results", bufs=8))
         psum = ctx.enter_context(tc.psum_pool(name="psum", bufs=8))
 
         src_list = keep.tile([P, J // 16], U16, name="src_list")
@@ -62,22 +63,24 @@ def tile_list_rgg_ownL_kernel(
         make_identity(nc, ident[:])
         nc.gpsimd.memset(wgo_rows[:], 0.0)
         warm = keep.tile([P, 1], F32, name="warm")
-        nc.scalar.activation(warm[:], ident[:, 0:1], SIGMOID)
+        warmed = keep.tile([P, 1], F32, name="warmed")
+        nc.vector.memset(warm[:], 0.0)
+        nc.scalar.activation(warmed[:], warm[:], SIGMOID)
         for tile in out_rows:
             nc.gpsimd.memset(tile[:], 0.0)
         nc.sync.dma_start(dst_list[:], offs2)
         for q in range(4):
             load_scale_quadrant(nc, tab_s, tab_scales, q)
         nc.sync.dma_start(src_list[:], offs)
-        load_scale_quadrant(nc, wb_s, wb_scales, 0)
-        nc.sync.dma_start(out=tab_w[:], in_=tab_words[0].rearrange("p t i -> p (t i)").bitcast(I32))
         nc.sync.dma_start(out=wa_raw[:], in_=wa.rearrange("(p i) n -> p i n", i=PACK))
-        for q in range(1, 4):
+        nc.sync.dma_start(out=tab_w[:], in_=tab_words[0].rearrange("p t i -> p (t i)").bitcast(I32))
+        for q in range(4):
             load_scale_quadrant(nc, wb_s, wb_scales, q)
-        for q in range(3):
+        for q in range(2):
             load_scale_quadrant(nc, wc_s, wc_scales, q)
         nc.sync.dma_start(out=wo_raw[:], in_=wo.rearrange("(p i) n -> p i n", i=PACK))
-        load_scale_quadrant(nc, wc_s, wc_scales, 3)
+        for q in range(2, 4):
+            load_scale_quadrant(nc, wc_s, wc_scales, q)
         nc.sync.dma_start(out=wb_w[:], in_=wb_words[0].bitcast(I32))
         nc.sync.dma_start(out=wc_w[:], in_=wc_words[0].rearrange("p n i -> p (n i)").bitcast(I32))
         nc.sync.dma_start(out=wgo_rows[0:EDGE_TILES, :], in_=wgo[0].rearrange("(e p) -> e p", p=P))
@@ -149,48 +152,42 @@ def tile_list_rgg_ownL_kernel(
         def gather_state(b):
             nc.vector.tensor_copy(picked[b][:], r_rows[b][:].indirect(dst_list[:]))
 
-        def finish(b, h):
+        def finish(b, tiles):
             rows = slice(b * P, (b + 1) * P)
+            width = len(tiles) * P
             turned = psum.tile([P, BANK], F32, name="bank")
-            state = ring.tile([P, BANK], F32, name="state")
-            for q in range(TILES_PER_HALF):
-                e = h * TILES_PER_HALF + q
+            state = ring.tile([P, width], F32, name="state")
+            for q, e in enumerate(tiles):
                 nc.tensor.transpose(turned[:, q * P : (q + 1) * P], picked[b][:, e * P : (e + 1) * P], ident[:])
-            for q in range(TILES_PER_HALF):
-                e = h * TILES_PER_HALF + q
+            for q, e in enumerate(tiles):
                 cols = slice(q * P, (q + 1) * P)
                 nc.scalar.activation(state[:, cols], turned[:, cols], COPY, scale=wgo_cols[:, e : e + 1])
             total = psum.tile([P, BANK], F32, name="bank")
-            for q in range(TILES_PER_HALF):
-                e = h * TILES_PER_HALF + q
+            for q, e in enumerate(tiles):
                 cols = slice(q * P, (q + 1) * P)
                 terms = (own[e][:, rows], message[e][:, rows], state[:, cols])
                 for i, term in enumerate(terms):
                     nc.tensor.matmul(
                         total[:, cols], term, ident[:], start=(i == 0), stop=(i == len(terms) - 1), is_transpose=True
                     )
-            result = ring.tile([P, BANK], F32, name="result")
-            nc.scalar.copy(out=result[:], in_=total[:])
-            offsets = dst_list[:, h * LIST_COLS_PER_HALF : (h + 1) * LIST_COLS_PER_HALF]
-            nc.vector.tensor_copy(out_rows[b % OUT_TILES][:].indirect(offsets), result[:])
+            result = results.tile([P, width], F32, name="result")
+            nc.scalar.copy(out=result[:], in_=total[:, 0:width])
+            offsets = dst_list[:, tiles.start * P // 16 : tiles.stop * P // 16]
+            nc.vector.tensor_copy(out_rows[b][:].indirect(offsets), result[:])
 
-        def store(b):
-            nc.sync.dma_start(out=out[b * P : (b + 1) * P, :], in_=out_rows[b % OUT_TILES][:])
-
+        first, last = range(0, 4), range(4, 8)
         gather_state(0)
-        for e in range(TILES_PER_HALF):
+        for e in first:
             edge_tile(e)
         gather_state(1)
-        finish(0, 0)
+        finish(0, first)
         gather_state(2)
-        finish(1, 0)
+        finish(1, first)
         gather_state(3)
-        for e in range(TILES_PER_HALF, EDGE_TILES):
+        for e in last:
             edge_tile(e)
-        finish(2, 0)
-        for b in range(OUT_TILES):
-            finish(b, 1)
-            store(b)
-        finish(3, 0)
-        finish(3, 1)
-        store(3)
+        finish(2, first)
+        finish(3, first)
+        for b in range(ROW_BLOCKS):
+            finish(b, last)
+            nc.sync.dma_start(out=out[b * P : (b + 1) * P, :], in_=out_rows[b][:])

@@ -26,7 +26,7 @@ ROW_BLOCKS = N // P
 HALVES = J // BANK
 TILES_PER_HALF = BANK // P
 LIST_COLS_PER_HALF = BANK // 16
-OUT_TILES = 4
+OUT_TILES = 2
 
 
 def load_scale_quadrant(nc, plane, scales, q):
@@ -41,8 +41,8 @@ def tile_list_rgg_ownL_kernel(
     with ExitStack() as ctx:
         keep = ctx.enter_context(tc.tile_pool(name="keep", bufs=1))
         ring = ctx.enter_context(tc.tile_pool(name="ring", bufs=3))
-        results = ctx.enter_context(tc.tile_pool(name="results", bufs=8))
-        psum = ctx.enter_context(tc.psum_pool(name="psum", bufs=8))
+        results = ctx.enter_context(tc.tile_pool(name="results", bufs=4))
+        psum = ctx.enter_context(tc.psum_pool(name="psum", bufs=1))
 
         src_list = keep.tile([P, J // 16], U16, name="src_list")
         dst_list = keep.tile([P, J // 16], U16, name="dst_list")
@@ -75,16 +75,17 @@ def tile_list_rgg_ownL_kernel(
         nc.sync.dma_start(out=wa_raw[:], in_=wa.rearrange("(p i) n -> p i n", i=PACK))
         nc.sync.dma_start(out=tab_w[:], in_=tab_words[0].rearrange("p t i -> p (t i)").bitcast(I32))
         for q in range(4):
-            load_scale_quadrant(nc, wb_s, wb_scales, q)
-        for q in range(2):
             load_scale_quadrant(nc, wc_s, wc_scales, q)
+        for q in range(2):
+            load_scale_quadrant(nc, wb_s, wb_scales, q)
         nc.sync.dma_start(out=wo_raw[:], in_=wo.rearrange("(p i) n -> p i n", i=PACK))
         for q in range(2, 4):
-            load_scale_quadrant(nc, wc_s, wc_scales, q)
-        nc.sync.dma_start(out=wb_w[:], in_=wb_words[0].bitcast(I32))
+            load_scale_quadrant(nc, wb_s, wb_scales, q)
         nc.sync.dma_start(out=wc_w[:], in_=wc_words[0].rearrange("p n i -> p (n i)").bitcast(I32))
-        nc.sync.dma_start(out=wgo_rows[0:EDGE_TILES, :], in_=wgo[0].rearrange("(e p) -> e p", p=P))
+        nc.sync.dma_start(out=wb_w[:], in_=wb_words[0].bitcast(I32))
         for b in range(ROW_BLOCKS):
+            if b == 2:
+                nc.sync.dma_start(out=wgo_rows[0:EDGE_TILES, :], in_=wgo[0].rearrange("(e p) -> e p", p=P))
             nc.sync.dma_start(out=r_rows[b][:], in_=rT[b * P : (b + 1) * P, :])
 
         src_w = keep.tile([P, J], U32, name="src_w", align_bytes=64)
@@ -109,85 +110,71 @@ def tile_list_rgg_ownL_kernel(
             nc.vector.quantize_mx(
                 out=codes[:].bitcast(FP8X4), scales=plane[:], in_=grouped[:].rearrange("p n i -> p (n i)")
             )
-            quantised.append((codes[:].bitcast(FP8X4), plane[:]))
+            quantised.append((codes[:], plane[:], FP8X4))
         wa_mx, wo_mx = quantised
-        wb_mx = (wb_w[:].bitcast(U8).bitcast(FP4X4), wb_s[:].bitcast(U8))
-        wc_mx = (wc_w[:].bitcast(FP8X4), wc_s[:].bitcast(U8))
+        wb_mx = (wb_w[:].bitcast(U8), wb_s[:].bitcast(U8), FP4X4)
+        wc_mx = (wc_w[:], wc_s[:].bitcast(U8), FP8X4)
 
-        wgo_bank = psum.tile([P, BANK], F32, name="bank")
+        wgo_bank = psum.tile([P, BANK], F32, name="back", bufs=2)
         nc.tensor.transpose(wgo_bank[:, 0:P], wgo_rows[:], ident[:])
         nc.scalar.copy(out=wgo_cols[:], in_=wgo_bank[:, 0:EDGE_TILES])
 
-        message = [keep.tile([P, N], F32, name=f"message{e}") for e in range(EDGE_TILES)]
-        own = [keep.tile([P, N], F32, name=f"own{e}") for e in range(EDGE_TILES)]
-        picked = [keep.tile([P, J], F32, name=f"picked{b}") for b in range(ROW_BLOCKS)]
+        picked = [[keep.tile([P, BANK], F32, name=f"picked{b}_{h}") for h in range(HALVES)] for b in range(ROW_BLOCKS)]
 
-        def mx_pass(bank, words, plane, e, weight, start, stop):
-            cols = slice(e * P, (e + 1) * P)
+        def mx_pass(bank, weight, width, b, words, plane, h, start, stop):
+            cols = slice(h * BANK, (h + 1) * BANK)
             nc.tensor.matmul_mx(
                 out=bank[:],
-                lhsT=words[:, cols].bitcast(FP8X4),
-                lhsT_scale=plane[:, cols],
-                rhs=weight[0],
-                rhs_scale=weight[1],
+                lhsT=weight[0][:, b * width : (b + 1) * width].bitcast(weight[2]),
+                lhsT_scale=weight[1][:, b * P : (b + 1) * P],
+                rhs=words[:, cols].bitcast(FP8X4),
+                rhs_scale=plane[:, cols],
                 start=start,
                 stop=stop,
             )
 
-        def edge_tile(e):
-            za = psum.tile([P, BANK], F32, name="bank")
-            mx_pass(za, dst_w, dst_s, e, wa_mx, True, False)
-            mx_pass(za, src_w, src_s, e, wb_mx, False, True)
-            ms = psum.tile([P, BANK], F32, name="bank")
-            mx_pass(ms, src_w, src_s, e, wc_mx, True, True)
-            ow = psum.tile([P, BANK], F32, name="bank")
-            mx_pass(ow, dst_w, dst_s, e, wo_mx, True, True)
-            eta = ring.tile([P, N], F32, name="eta")
+        def unit(b, h):
+            za = psum.tile([P, BANK], F32, name="za")
+            mx_pass(za, wa_mx, P, b, dst_w, dst_s, h, True, False)
+            mx_pass(za, wb_mx, 2 * P, b, src_w, src_s, h, False, True)
+            ms = psum.tile([P, BANK], F32, name="ms")
+            mx_pass(ms, wc_mx, P, b, src_w, src_s, h, True, True)
+            ow = psum.tile([P, BANK], F32, name="ow")
+            mx_pass(ow, wo_mx, P, b, dst_w, dst_s, h, True, True)
+            eta = ring.tile([P, BANK], F32, name="eta")
             nc.scalar.activation(eta[:], za[:], SIGMOID)
-            weighted = ring.tile([P, N], F32, name="weighted")
-            nc.scalar.activation(weighted[:], ms[:], COPY, scale=wgo_cols[:, e : e + 1])
-            nc.gpsimd.tensor_tensor(message[e][:], weighted[:], eta[:], MULT)
-            nc.scalar.activation(own[e][:], ow[:], COPY, scale=wgo_cols[:, e : e + 1])
+            source = ring.tile([P, BANK], F32, name="source")
+            nc.scalar.copy(out=source[:], in_=ms[:])
+            message = ring.tile([P, BANK], F32, name="message")
+            nc.gpsimd.tensor_tensor(message[:], source[:], eta[:], MULT)
+            own = ring.tile([P, BANK], F32, name="own")
+            nc.scalar.copy(out=own[:], in_=ow[:])
 
-        def gather_state(b):
-            nc.vector.tensor_copy(picked[b][:], r_rows[b][:].indirect(dst_list[:]))
-
-        def finish(b, tiles):
-            rows = slice(b * P, (b + 1) * P)
-            width = len(tiles) * P
-            turned = psum.tile([P, BANK], F32, name="bank")
-            state = ring.tile([P, width], F32, name="state")
-            for q, e in enumerate(tiles):
-                nc.tensor.transpose(turned[:, q * P : (q + 1) * P], picked[b][:, e * P : (e + 1) * P], ident[:])
-            for q, e in enumerate(tiles):
+            total = psum.tile([P, BANK], F32, name="total", bufs=3)
+            terms = (message, own, picked[b][h])
+            for q in range(TILES_PER_HALF):
                 cols = slice(q * P, (q + 1) * P)
-                nc.scalar.activation(state[:, cols], turned[:, cols], COPY, scale=wgo_cols[:, e : e + 1])
-            total = psum.tile([P, BANK], F32, name="bank")
-            for q, e in enumerate(tiles):
-                cols = slice(q * P, (q + 1) * P)
-                terms = (own[e][:, rows], message[e][:, rows], state[:, cols])
                 for i, term in enumerate(terms):
                     nc.tensor.matmul(
-                        total[:, cols], term, ident[:], start=(i == 0), stop=(i == len(terms) - 1), is_transpose=True
+                        total[:, cols], term[:, cols], ident[:], start=(i == 0), stop=(i == len(terms) - 1), is_transpose=True
                     )
-            result = results.tile([P, width], F32, name="result")
-            nc.scalar.copy(out=result[:], in_=total[:, 0:width])
-            offsets = dst_list[:, tiles.start * P // 16 : tiles.stop * P // 16]
-            nc.vector.tensor_copy(out_rows[b][:].indirect(offsets), result[:])
+            weighted = ring.tile([P, BANK], F32, name="weighted")
+            for q in range(TILES_PER_HALF):
+                cols = slice(q * P, (q + 1) * P)
+                e = h * TILES_PER_HALF + q
+                nc.scalar.activation(weighted[:, cols], total[:, cols], COPY, scale=wgo_cols[:, e : e + 1])
+            back = psum.tile([P, BANK], F32, name="back", bufs=2)
+            for q in range(TILES_PER_HALF):
+                cols = slice(q * P, (q + 1) * P)
+                nc.tensor.transpose(back[:, cols], weighted[:, cols], ident[:])
+            result = results.tile([P, BANK], F32, name="result")
+            nc.scalar.copy(out=result[:], in_=back[:])
+            nc.vector.tensor_copy(out_rows[b % OUT_TILES][:].indirect(half_list(dst_list, h)), result[:])
 
-        first, last = range(0, 4), range(4, 8)
-        gather_state(0)
-        for e in first:
-            edge_tile(e)
-        gather_state(1)
-        finish(0, first)
-        gather_state(2)
-        finish(1, first)
-        gather_state(3)
-        for e in last:
-            edge_tile(e)
-        finish(2, first)
-        finish(3, first)
         for b in range(ROW_BLOCKS):
-            finish(b, last)
-            nc.sync.dma_start(out=out[b * P : (b + 1) * P, :], in_=out_rows[b][:])
+            for h in range(HALVES):
+                nc.vector.tensor_copy(picked[b][h][:], r_rows[b][:].indirect(half_list(dst_list, h)))
+        for b in range(ROW_BLOCKS):
+            for h in range(HALVES):
+                unit(b, h)
+            nc.sync.dma_start(out=out[b * P : (b + 1) * P, :], in_=out_rows[b % OUT_TILES][:])

@@ -26,12 +26,13 @@ ROW_BLOCKS = N // P
 HALVES = J // BANK
 TILES_PER_HALF = BANK // P
 LIST_COLS_PER_HALF = BANK // 16
-OUT_TILES = 2
+OUT_TILES = 3
+AHEAD = 2
 
 
 def load_scale_quadrant(nc, plane, scales, q):
     rows = scales[0].bitcast(I32)
-    nc.sync.dma_start(out=plane[32 * q : 32 * (q + 1), :], in_=rows[4 * q : 4 * q + 4, :].partition_broadcast(8))
+    nc.sync.dma_start(out=plane[32 * q : 32 * q + 4, :], in_=rows[4 * q : 4 * q + 4, :])
 
 
 def tile_list_rgg_ownL_kernel(
@@ -40,7 +41,7 @@ def tile_list_rgg_ownL_kernel(
     nc = tc.nc
     with ExitStack() as ctx:
         keep = ctx.enter_context(tc.tile_pool(name="keep", bufs=1))
-        ring = ctx.enter_context(tc.tile_pool(name="ring", bufs=3))
+        ring = ctx.enter_context(tc.tile_pool(name="ring", bufs=4))
         results = ctx.enter_context(tc.tile_pool(name="results", bufs=4))
         psum = ctx.enter_context(tc.psum_pool(name="psum", bufs=1))
 
@@ -60,6 +61,8 @@ def tile_list_rgg_ownL_kernel(
         r_rows = [keep.tile([P, T], F32, name=f"r_rows{b}") for b in range(ROW_BLOCKS)]
         out_rows = [keep.tile([P, T], F32, name=f"out_rows{i}") for i in range(OUT_TILES)]
 
+        for plane in (tab_s, wc_s, wb_s):
+            nc.gpsimd.memset(plane[:], 0)
         make_identity(nc, ident[:])
         nc.gpsimd.memset(wgo_rows[:], 0.0)
         warm = keep.tile([P, 1], F32, name="warm")
@@ -106,7 +109,10 @@ def tile_list_rgg_ownL_kernel(
             grouped = keep.tile([P, N, PACK], BF16, name=f"{label}_grouped", align_bytes=64)
             codes = keep.tile([P, N], U32, name=f"{label}_codes", align_bytes=64)
             plane = keep.tile([P, N], U8, name=f"{label}_plane", align_bytes=64)
-            nc.scalar.copy(out=grouped[:], in_=raw[:].rearrange("p i n -> p n i"))
+            nc.scalar.copy(
+                out=grouped[:].rearrange("p (c n) i -> p c i n", n=PACK),
+                in_=raw[:].rearrange("p i (c n) -> p c i n", n=PACK),
+            )
             nc.vector.quantize_mx(
                 out=codes[:].bitcast(FP8X4), scales=plane[:], in_=grouped[:].rearrange("p n i -> p (n i)")
             )
@@ -119,7 +125,7 @@ def tile_list_rgg_ownL_kernel(
         nc.tensor.transpose(wgo_bank[:, 0:P], wgo_rows[:], ident[:])
         nc.scalar.copy(out=wgo_cols[:], in_=wgo_bank[:, 0:EDGE_TILES])
 
-        picked = [[keep.tile([P, BANK], F32, name=f"picked{b}_{h}") for h in range(HALVES)] for b in range(ROW_BLOCKS)]
+        picked = [keep.tile([P, J], F32, name=f"picked{b}") for b in range(ROW_BLOCKS)]
 
         def mx_pass(bank, weight, width, b, words, plane, h, start, stop):
             cols = slice(h * BANK, (h + 1) * BANK)
@@ -149,9 +155,11 @@ def tile_list_rgg_ownL_kernel(
             nc.gpsimd.tensor_tensor(message[:], source[:], eta[:], MULT)
             own = ring.tile([P, BANK], F32, name="own")
             nc.scalar.copy(out=own[:], in_=ow[:])
+            return message, own
 
+        def finish(b, h, message, own):
             total = psum.tile([P, BANK], F32, name="total", bufs=3)
-            terms = (message, own, picked[b][h])
+            terms = (message, own, picked[b][:, h * BANK : (h + 1) * BANK])
             for q in range(TILES_PER_HALF):
                 cols = slice(q * P, (q + 1) * P)
                 for i, term in enumerate(terms):
@@ -172,9 +180,21 @@ def tile_list_rgg_ownL_kernel(
             nc.vector.tensor_copy(out_rows[b % OUT_TILES][:].indirect(half_list(dst_list, h)), result[:])
 
         for b in range(ROW_BLOCKS):
-            for h in range(HALVES):
-                nc.vector.tensor_copy(picked[b][h][:], r_rows[b][:].indirect(half_list(dst_list, h)))
-        for b in range(ROW_BLOCKS):
-            for h in range(HALVES):
-                unit(b, h)
-            nc.sync.dma_start(out=out[b * P : (b + 1) * P, :], in_=out_rows[b % OUT_TILES][:])
+            nc.vector.tensor_copy(picked[b][:], r_rows[b][:].indirect(dst_list[:]))
+        def store(b):
+            rows = slice(b * P, (b + 1) * P)
+            tile = out_rows[b % OUT_TILES]
+            if b < ROW_BLOCKS - 1:
+                nc.sync.dma_start(out=out[rows, :], in_=tile[:])
+            else:
+                nc.sync.dma_start(out=out[rows, 0 : T // 2], in_=tile[:, 0 : T // 2])
+                nc.scalar.dma_start(out=out[rows, T // 2 : T], in_=tile[:, T // 2 : T])
+
+        units = [(pair + i, h) for pair in range(0, ROW_BLOCKS, 2) for h in range(HALVES) for i in range(2)]
+        staged = [unit(b, h) for b, h in units[:AHEAD]]
+        for u, (b, h) in enumerate(units):
+            finish(b, h, *staged[u])
+            if h == HALVES - 1:
+                store(b)
+            if u + AHEAD < len(units):
+                staged.append(unit(*units[u + AHEAD]))

@@ -69,7 +69,8 @@ def tile_list_rgg_ownL_kernel(
         warmed = keep.tile([P, 1], F32, name="warmed")
         nc.vector.memset(warm[:], 0.0)
         nc.scalar.activation(warmed[:], warm[:], SIGMOID)
-        for tile in out_rows:
+        nc.vector.memset(out_rows[0][:].bitcast(I32), 0)
+        for tile in out_rows[1:]:
             nc.gpsimd.memset(tile[:], 0.0)
         nc.sync.dma_start(dst_list[:], offs2)
         for q in range(4):
@@ -87,7 +88,7 @@ def tile_list_rgg_ownL_kernel(
         nc.sync.dma_start(out=wc_w[:], in_=wc_words[0].rearrange("p n i -> p (n i)").bitcast(I32))
         nc.sync.dma_start(out=wb_w[:], in_=wb_words[0].bitcast(I32))
         for b in range(ROW_BLOCKS):
-            if b == 2:
+            if b == 3:
                 nc.sync.dma_start(out=wgo_rows[0:EDGE_TILES, :], in_=wgo[0].rearrange("(e p) -> e p", p=P))
             nc.sync.dma_start(out=r_rows[b][:], in_=rT[b * P : (b + 1) * P, :])
 

@@ -42,7 +42,6 @@ def tile_list_rgg_ownL_kernel(
     with ExitStack() as ctx:
         keep = ctx.enter_context(tc.tile_pool(name="keep", bufs=1))
         ring = ctx.enter_context(tc.tile_pool(name="ring", bufs=4))
-        results = ctx.enter_context(tc.tile_pool(name="results", bufs=4))
         psum = ctx.enter_context(tc.psum_pool(name="psum", bufs=1))
 
         src_list = keep.tile([P, J // 16], U16, name="src_list")
@@ -88,7 +87,7 @@ def tile_list_rgg_ownL_kernel(
         nc.sync.dma_start(out=wc_w[:], in_=wc_words[0].rearrange("p n i -> p (n i)").bitcast(I32))
         nc.sync.dma_start(out=wb_w[:], in_=wb_words[0].bitcast(I32))
         for b in range(ROW_BLOCKS):
-            if b == 3:
+            if b == 2:
                 nc.sync.dma_start(out=wgo_rows[0:EDGE_TILES, :], in_=wgo[0].rearrange("(e p) -> e p", p=P))
             nc.sync.dma_start(out=r_rows[b][:], in_=rT[b * P : (b + 1) * P, :])
 
@@ -107,7 +106,7 @@ def tile_list_rgg_ownL_kernel(
             cols = slice(h * BANK, (h + 1) * BANK)
             nc.vector.tensor_copy(dst_w[:, cols], tab_w[:].bitcast(U32).indirect(half_list(dst_list, h)))
             nc.vector.tensor_copy(src_w[:, cols], tab_w[:].bitcast(U32).indirect(half_list(src_list, h)))
-            grouped = keep.tile([P, N, PACK], BF16, name=f"{label}_grouped", align_bytes=64)
+            grouped = keep.tile([P, N, PACK], BF16, name="grouped", tag=f"{label}_grouped", align_bytes=64)
             codes = keep.tile([P, N], U32, name=f"{label}_codes", align_bytes=64)
             plane = keep.tile([P, N], U8, name=f"{label}_plane", align_bytes=64)
             nc.scalar.copy(
@@ -127,6 +126,8 @@ def tile_list_rgg_ownL_kernel(
         nc.scalar.copy(out=wgo_cols[:], in_=wgo_bank[:, 0:EDGE_TILES])
 
         picked = [keep.tile([P, J], F32, name=f"picked{b}") for b in range(ROW_BLOCKS)]
+
+        result = [keep.tile([P, J], F32, name=f"result{b}") for b in range(ROW_BLOCKS)]
 
         def mx_pass(bank, weight, width, b, words, plane, h, start, stop):
             cols = slice(h * BANK, (h + 1) * BANK)
@@ -152,7 +153,10 @@ def tile_list_rgg_ownL_kernel(
             nc.scalar.activation(eta[:], za[:], SIGMOID)
             source = ring.tile([P, BANK], F32, name="source")
             nc.scalar.copy(out=source[:], in_=ms[:])
-            message = ring.tile([P, BANK], F32, name="message")
+            if (b, h) == (0, 0):
+                message = keep.tile([P, BANK], F32, name="first_message", tag="wo_grouped", align_bytes=64)
+            else:
+                message = ring.tile([P, BANK], F32, name="message")
             nc.gpsimd.tensor_tensor(message[:], source[:], eta[:], MULT)
             own = ring.tile([P, BANK], F32, name="own")
             nc.scalar.copy(out=own[:], in_=ow[:])
@@ -176,11 +180,19 @@ def tile_list_rgg_ownL_kernel(
             for q in range(TILES_PER_HALF):
                 cols = slice(q * P, (q + 1) * P)
                 nc.tensor.transpose(back[:, cols], weighted[:, cols], ident[:])
-            result = results.tile([P, BANK], F32, name="result")
-            nc.scalar.copy(out=result[:], in_=back[:])
-            nc.vector.tensor_copy(out_rows[b % OUT_TILES][:].indirect(half_list(dst_list, h)), result[:])
+            cols = slice(h * BANK, (h + 1) * BANK)
+            nc.scalar.copy(out=result[b][:, cols], in_=back[:])
+            window = out_rows[b % OUT_TILES][:]
+            if b < 2:
+                nc.vector.tensor_copy(window.indirect(half_list(dst_list, h)), result[b][:, cols])
+            elif h == HALVES - 1:
+                nc.vector.tensor_copy(window.indirect(dst_list[:]), result[b][:])
 
-        for b in range(ROW_BLOCKS):
+        for b in range(2):
+            for h in range(HALVES):
+                cols = slice(h * BANK, (h + 1) * BANK)
+                nc.vector.tensor_copy(picked[b][:, cols], r_rows[b][:].indirect(half_list(dst_list, h)))
+        for b in range(2, ROW_BLOCKS):
             nc.vector.tensor_copy(picked[b][:], r_rows[b][:].indirect(dst_list[:]))
         def store(b):
             rows = slice(b * P, (b + 1) * P)
@@ -191,7 +203,8 @@ def tile_list_rgg_ownL_kernel(
                 nc.sync.dma_start(out=out[rows, 0 : T // 2], in_=tile[:, 0 : T // 2])
                 nc.scalar.dma_start(out=out[rows, T // 2 : T], in_=tile[:, T // 2 : T])
 
-        units = [(pair + i, h) for pair in range(0, ROW_BLOCKS, 2) for h in range(HALVES) for i in range(2)]
+        units = [(b, h) for h in range(HALVES) for b in range(2)]
+        units.extend((b, h) for b in range(2, ROW_BLOCKS) for h in range(HALVES))
         staged = [unit(b, h) for b, h in units[:AHEAD]]
         for u, (b, h) in enumerate(units):
             finish(b, h, *staged[u])

@@ -30,9 +30,9 @@ OUT_TILES = 3
 AHEAD = 2
 
 
-def load_scale_quadrant(nc, plane, scales, q):
+def load_scale_quadrant(queue, plane, scales, q):
     rows = scales[0].bitcast(I32)
-    nc.sync.dma_start(out=plane[32 * q : 32 * q + 4, :], in_=rows[4 * q : 4 * q + 4, :])
+    queue.dma_start(out=plane[32 * q : 32 * q + 4, :], in_=rows[4 * q : 4 * q + 4, :])
 
 
 def tile_list_rgg_ownL_kernel(
@@ -57,11 +57,13 @@ def tile_list_rgg_ownL_kernel(
         wgo_rows = keep.tile([P, P], F32, name="wgo_rows")
         wgo_cols = keep.tile([P, EDGE_TILES], F32, name="wgo_cols")
         ident = keep.tile([P, P], F32, name="ident")
-        r_rows = [keep.tile([P, T], F32, name=f"r_rows{b}") for b in range(ROW_BLOCKS)]
-        out_rows = [keep.tile([P, T], F32, name=f"out_rows{i}") for i in range(OUT_TILES)]
+        r_rows = [keep.tile([P, T], F32, name=f"r_rows{b}", tag=f"r_rows{b}") for b in range(ROW_BLOCKS)]
+        out_rows = [keep.tile([P, T], F32, name=f"out_rows{i}") for i in range(OUT_TILES - 1)]
 
         for plane in (tab_s, wc_s, wb_s):
             nc.gpsimd.memset(plane[:], 0)
+        for q in range(4):
+            load_scale_quadrant(nc.gpsimd, wb_s, wb_scales, q)
         make_identity(nc, ident[:])
         nc.gpsimd.memset(wgo_rows[:], 0.0)
         warm = keep.tile([P, 1], F32, name="warm")
@@ -73,17 +75,13 @@ def tile_list_rgg_ownL_kernel(
             nc.gpsimd.memset(tile[:], 0.0)
         nc.sync.dma_start(dst_list[:], offs2)
         for q in range(4):
-            load_scale_quadrant(nc, tab_s, tab_scales, q)
+            load_scale_quadrant(nc.sync, tab_s, tab_scales, q)
         nc.sync.dma_start(src_list[:], offs)
         nc.sync.dma_start(out=wa_raw[:], in_=wa.rearrange("(p i) n -> p i n", i=PACK))
         nc.sync.dma_start(out=tab_w[:], in_=tab_words[0].rearrange("p t i -> p (t i)").bitcast(I32))
         for q in range(4):
-            load_scale_quadrant(nc, wc_s, wc_scales, q)
-        for q in range(2):
-            load_scale_quadrant(nc, wb_s, wb_scales, q)
+            load_scale_quadrant(nc.sync, wc_s, wc_scales, q)
         nc.sync.dma_start(out=wo_raw[:], in_=wo.rearrange("(p i) n -> p i n", i=PACK))
-        for q in range(2, 4):
-            load_scale_quadrant(nc, wb_s, wb_scales, q)
         nc.sync.dma_start(out=wc_w[:], in_=wc_words[0].rearrange("p n i -> p (n i)").bitcast(I32))
         nc.sync.dma_start(out=wb_w[:], in_=wb_words[0].bitcast(I32))
         for b in range(ROW_BLOCKS):
@@ -202,6 +200,9 @@ def tile_list_rgg_ownL_kernel(
             else:
                 nc.sync.dma_start(out=out[rows, 0 : T // 2], in_=tile[:, 0 : T // 2])
                 nc.scalar.dma_start(out=out[rows, T // 2 : T], in_=tile[:, T // 2 : T])
+
+        out_rows.append(keep.tile([P, T], F32, name="out_rows2", tag="r_rows2"))
+        nc.gpsimd.memset(out_rows[2][:], 0.0)
 
         units = [(b, h) for h in range(HALVES) for b in range(2)]
         units.extend((b, h) for b in range(2, ROW_BLOCKS) for h in range(HALVES))

@@ -69,13 +69,13 @@ def tile_list_rgg_ownL_kernel(
         warm = keep.tile([P, 1], F32, name="warm")
         warmed = keep.tile([P, 1], F32, name="warmed")
         nc.vector.memset(warm[:], 0.0)
-        nc.scalar.activation(warmed[:], warm[:], SIGMOID)
         nc.vector.memset(out_rows[0][:].bitcast(I32), 0)
         for tile in out_rows[1:]:
             nc.gpsimd.memset(tile[:], 0.0)
         nc.sync.dma_start(dst_list[:], offs2)
-        for q in range(4):
+        for q in (0, 2, 1, 3):
             load_scale_quadrant(nc.sync, tab_s, tab_scales, q)
+        nc.scalar.activation(warmed[:], warm[:], SIGMOID)
         nc.sync.dma_start(src_list[:], offs)
         nc.sync.dma_start(out=wa_raw[:], in_=wa.rearrange("(p i) n -> p i n", i=PACK))
         nc.sync.dma_start(out=tab_w[:], in_=tab_words[0].rearrange("p t i -> p (t i)").bitcast(I32))
@@ -139,6 +139,9 @@ def tile_list_rgg_ownL_kernel(
                 stop=stop,
             )
 
+        def parts(b, h):
+            return [(0, 1), (2, 3)] if (b, h) == (0, 0) else [(0, 1, 2, 3)]
+
         def unit(b, h):
             za = psum.tile([P, BANK], F32, name="za")
             mx_pass(za, wa_mx, P, b, dst_w, dst_s, h, True, False)
@@ -148,38 +151,42 @@ def tile_list_rgg_ownL_kernel(
             ow = psum.tile([P, BANK], F32, name="ow")
             mx_pass(ow, wo_mx, P, b, dst_w, dst_s, h, True, True)
             eta = ring.tile([P, BANK], F32, name="eta")
-            nc.scalar.activation(eta[:], za[:], SIGMOID)
             source = ring.tile([P, BANK], F32, name="source")
-            nc.scalar.copy(out=source[:], in_=ms[:])
             if (b, h) == (0, 0):
                 message = keep.tile([P, BANK], F32, name="first_message", tag="wo_grouped", align_bytes=64)
             else:
                 message = ring.tile([P, BANK], F32, name="message")
-            nc.gpsimd.tensor_tensor(message[:], source[:], eta[:], MULT)
+            for part in parts(b, h):
+                cols = slice(part[0] * P, (part[-1] + 1) * P)
+                nc.scalar.activation(eta[:, cols], za[:, cols], SIGMOID)
+                nc.scalar.copy(out=source[:, cols], in_=ms[:, cols])
+                nc.gpsimd.tensor_tensor(message[:, cols], source[:, cols], eta[:, cols], MULT)
             own = ring.tile([P, BANK], F32, name="own")
             nc.scalar.copy(out=own[:], in_=ow[:])
             return message, own
 
         def finish(b, h, message, own):
-            total = psum.tile([P, BANK], F32, name="total", bufs=3)
             terms = (message, own, picked[b][:, h * BANK : (h + 1) * BANK])
-            for q in range(TILES_PER_HALF):
-                cols = slice(q * P, (q + 1) * P)
-                for i, term in enumerate(terms):
-                    nc.tensor.matmul(
-                        total[:, cols], term[:, cols], ident[:], start=(i == 0), stop=(i == len(terms) - 1), is_transpose=True
-                    )
             weighted = ring.tile([P, BANK], F32, name="weighted")
-            for q in range(TILES_PER_HALF):
-                cols = slice(q * P, (q + 1) * P)
-                e = h * TILES_PER_HALF + q
-                nc.scalar.activation(weighted[:, cols], total[:, cols], COPY, scale=wgo_cols[:, e : e + 1])
-            back = psum.tile([P, BANK], F32, name="back", bufs=2)
-            for q in range(TILES_PER_HALF):
-                cols = slice(q * P, (q + 1) * P)
-                nc.tensor.transpose(back[:, cols], weighted[:, cols], ident[:])
+            for part in parts(b, h):
+                total = psum.tile([P, BANK], F32, name="total", bufs=3)
+                for q in part:
+                    cols = slice(q * P, (q + 1) * P)
+                    for i, term in enumerate(terms):
+                        nc.tensor.matmul(
+                            total[:, cols], term[:, cols], ident[:], start=(i == 0), stop=(i == len(terms) - 1), is_transpose=True
+                        )
+                for q in part:
+                    cols = slice(q * P, (q + 1) * P)
+                    e = h * TILES_PER_HALF + q
+                    nc.scalar.activation(weighted[:, cols], total[:, cols], COPY, scale=wgo_cols[:, e : e + 1])
+                back = psum.tile([P, BANK], F32, name="back", bufs=2)
+                for q in part:
+                    cols = slice(q * P, (q + 1) * P)
+                    nc.tensor.transpose(back[:, cols], weighted[:, cols], ident[:])
+                first, last = part[0] * P, (part[-1] + 1) * P
+                nc.scalar.copy(out=result[b][:, h * BANK + first : h * BANK + last], in_=back[:, first:last])
             cols = slice(h * BANK, (h + 1) * BANK)
-            nc.scalar.copy(out=result[b][:, cols], in_=back[:])
             window = out_rows[b % OUT_TILES][:]
             if b < 2:
                 nc.vector.tensor_copy(window.indirect(half_list(dst_list, h)), result[b][:, cols])

@@ -26,7 +26,7 @@ ROW_BLOCKS = N // P
 HALVES = J // BANK
 TILES_PER_HALF = BANK // P
 LIST_COLS_PER_HALF = BANK // 16
-OUT_TILES = 3
+OUT_TILES = 2
 AHEAD = 2
 
 
@@ -58,7 +58,7 @@ def tile_list_rgg_ownL_kernel(
         wgo_cols = keep.tile([P, EDGE_TILES], F32, name="wgo_cols")
         ident = keep.tile([P, P], F32, name="ident")
         r_rows = [keep.tile([P, T], F32, name=f"r_rows{b}", tag=f"r_rows{b}") for b in range(ROW_BLOCKS)]
-        out_rows = [keep.tile([P, T], F32, name=f"out_rows{i}") for i in range(OUT_TILES - 1)]
+        out_rows = [keep.tile([P, T], F32, name=f"out_rows{i}") for i in range(OUT_TILES)]
 
         for plane in (tab_s, wc_s, wb_s):
             nc.gpsimd.memset(plane[:], 0)
@@ -69,9 +69,8 @@ def tile_list_rgg_ownL_kernel(
         warm = keep.tile([P, 1], F32, name="warm")
         warmed = keep.tile([P, 1], F32, name="warmed")
         nc.vector.memset(warm[:], 0.0)
-        nc.vector.memset(out_rows[0][:].bitcast(I32), 0)
-        for tile in out_rows[1:]:
-            nc.gpsimd.memset(tile[:], 0.0)
+        for tile in out_rows:
+            nc.vector.memset(tile[:].bitcast(I32), 0)
         nc.sync.dma_start(dst_list[:], offs2)
         for q in (0, 2, 1, 3):
             load_scale_quadrant(nc.sync, tab_s, tab_scales, q)
@@ -188,16 +187,16 @@ def tile_list_rgg_ownL_kernel(
                 nc.scalar.copy(out=result[b][:, h * BANK + first : h * BANK + last], in_=back[:, first:last])
             cols = slice(h * BANK, (h + 1) * BANK)
             window = out_rows[b % OUT_TILES][:]
-            if b < 2:
+            if b < 1:
                 nc.vector.tensor_copy(window.indirect(half_list(dst_list, h)), result[b][:, cols])
             elif h == HALVES - 1:
                 nc.vector.tensor_copy(window.indirect(dst_list[:]), result[b][:])
 
-        for b in range(2):
+        for b in range(1):
             for h in range(HALVES):
                 cols = slice(h * BANK, (h + 1) * BANK)
                 nc.vector.tensor_copy(picked[b][:, cols], r_rows[b][:].indirect(half_list(dst_list, h)))
-        for b in range(2, ROW_BLOCKS):
+        for b in range(1, ROW_BLOCKS):
             nc.vector.tensor_copy(picked[b][:], r_rows[b][:].indirect(dst_list[:]))
         def store(b):
             rows = slice(b * P, (b + 1) * P)
@@ -208,11 +207,8 @@ def tile_list_rgg_ownL_kernel(
                 nc.sync.dma_start(out=out[rows, 0 : T // 2], in_=tile[:, 0 : T // 2])
                 nc.scalar.dma_start(out=out[rows, T // 2 : T], in_=tile[:, T // 2 : T])
 
-        out_rows.append(keep.tile([P, T], F32, name="out_rows2", tag="r_rows2"))
-        nc.gpsimd.memset(out_rows[2][:], 0.0)
 
-        units = [(b, h) for h in range(HALVES) for b in range(2)]
-        units.extend((b, h) for b in range(2, ROW_BLOCKS) for h in range(HALVES))
+        units = [(b, h) for b in range(ROW_BLOCKS) for h in range(HALVES)]
         staged = [unit(b, h) for b, h in units[:AHEAD]]
         for u, (b, h) in enumerate(units):
             finish(b, h, *staged[u])

@@ -28,6 +28,7 @@ TILES_PER_HALF = BANK // P
 LIST_COLS_PER_HALF = BANK // 16
 OUT_TILES = 2
 AHEAD = 2
+FIRST_PART = 2 * P
 
 
 def load_scale_quadrant(queue, plane, scales, q):
@@ -188,7 +189,8 @@ def tile_list_rgg_ownL_kernel(
             cols = slice(h * BANK, (h + 1) * BANK)
             window = out_rows[b % OUT_TILES][:]
             if b < 1:
-                nc.vector.tensor_copy(window.indirect(half_list(dst_list, h)), result[b][:, cols])
+                first, last = (0, FIRST_PART) if h == 0 else (FIRST_PART, J)
+                nc.vector.tensor_copy(window.indirect(dst_list[:, first // 16 : last // 16]), result[b][:, first:last])
             elif h == HALVES - 1:
                 nc.vector.tensor_copy(window.indirect(dst_list[:]), result[b][:])
 

@@ -28,6 +28,7 @@ TILES_PER_HALF = BANK // P
 LIST_COLS_PER_HALF = BANK // 16
 OUT_TILES = 2
 AHEAD = 2
+STORE_PIECES = (1, 2, 4, 4)
 FIRST_PART = 2 * P
 
 
@@ -53,7 +54,7 @@ def tile_list_rgg_ownL_kernel(
         wb_s = keep.tile([P, N // 4], I32, name="wb_s", align_bytes=64)
         wc_w = keep.tile([P, N], I32, name="wc_w", align_bytes=64)
         wc_s = keep.tile([P, N // 4], I32, name="wc_s", align_bytes=64)
-        wa_raw = keep.tile([P, PACK, N], F32, name="wa_raw")
+        wa_raw = [keep.tile([P, PACK, N // 2], F32, name=f"wa_raw{i}", tag=f"wa_raw{i}", align_bytes=64) for i in range(2)]
         wo_raw = keep.tile([P, PACK, N], F32, name="wo_raw")
         wgo_rows = keep.tile([P, P], F32, name="wgo_rows")
         wgo_cols = keep.tile([P, EDGE_TILES], F32, name="wgo_cols")
@@ -77,8 +78,10 @@ def tile_list_rgg_ownL_kernel(
             load_scale_quadrant(nc.sync, tab_s, tab_scales, q)
         nc.scalar.activation(warmed[:], warm[:], SIGMOID)
         nc.sync.dma_start(src_list[:], offs)
-        nc.sync.dma_start(out=wa_raw[:], in_=wa.rearrange("(p i) n -> p i n", i=PACK))
+        wa_rows = wa.rearrange("(p i) n -> p i n", i=PACK)
+        nc.sync.dma_start(out=wa_raw[0][:], in_=wa_rows[:, :, 0 : N // 2])
         nc.sync.dma_start(out=tab_w[:], in_=tab_words[0].rearrange("p t i -> p (t i)").bitcast(I32))
+        nc.sync.dma_start(out=wa_raw[1][:], in_=wa_rows[:, :, N // 2 : N])
         for q in range(4):
             load_scale_quadrant(nc.sync, wc_s, wc_scales, q)
         nc.sync.dma_start(out=wo_raw[:], in_=wo.rearrange("(p i) n -> p i n", i=PACK))
@@ -89,9 +92,7 @@ def tile_list_rgg_ownL_kernel(
                 nc.sync.dma_start(out=wgo_rows[0:EDGE_TILES, :], in_=wgo[0].rearrange("(e p) -> e p", p=P))
             nc.sync.dma_start(out=r_rows[b][:], in_=rT[b * P : (b + 1) * P, :])
 
-        src_w = keep.tile([P, J], U32, name="src_w", align_bytes=64)
         src_s = keep.tile([P, J], U8, name="src_s", align_bytes=64)
-        dst_w = keep.tile([P, J], U32, name="dst_w", align_bytes=64)
         dst_s = keep.tile([P, J], U8, name="dst_s", align_bytes=64)
         nc.vector.tensor_copy(dst_s[:], tab_s[:].bitcast(U8).indirect(dst_list[:]))
         nc.vector.tensor_copy(src_s[:], tab_s[:].bitcast(U8).indirect(src_list[:]))
@@ -99,18 +100,22 @@ def tile_list_rgg_ownL_kernel(
         def half_list(lst, h):
             return lst[:, h * LIST_COLS_PER_HALF : (h + 1) * LIST_COLS_PER_HALF]
 
-        quantised = []
-        for h, (label, raw) in enumerate((("wa", wa_raw), ("wo", wo_raw))):
-            cols = slice(h * BANK, (h + 1) * BANK)
-            nc.vector.tensor_copy(dst_w[:, cols], tab_w[:].bitcast(U32).indirect(half_list(dst_list, h)))
-            nc.vector.tensor_copy(src_w[:, cols], tab_w[:].bitcast(U32).indirect(half_list(src_list, h)))
+        quantised, dst_w, src_w = [], [], []
+        for h, (label, raw) in enumerate((("wa", wa_raw), ("wo", [wo_raw]))):
+            both = keep.tile([P, 2 * BANK], U32, name="both", tag=("first_words", "wa_raw1")[h], align_bytes=64)
+            dst_w.append(both[:, 0:BANK])
+            src_w.append(both[:, BANK : 2 * BANK])
+            nc.vector.tensor_copy(dst_w[h], tab_w[:].bitcast(U32).indirect(half_list(dst_list, h)))
+            nc.vector.tensor_copy(src_w[h], tab_w[:].bitcast(U32).indirect(half_list(src_list, h)))
             grouped = keep.tile([P, N, PACK], BF16, name="grouped", tag=f"{label}_grouped", align_bytes=64)
             codes = keep.tile([P, N], U32, name=f"{label}_codes", align_bytes=64)
             plane = keep.tile([P, N], U8, name=f"{label}_plane", align_bytes=64)
-            nc.scalar.copy(
-                out=grouped[:].rearrange("p (c n) i -> p c i n", n=PACK),
-                in_=raw[:].rearrange("p i (c n) -> p c i n", n=PACK),
-            )
+            width = N // len(raw)
+            for i, piece in enumerate(raw):
+                nc.scalar.copy(
+                    out=grouped[:, i * width : (i + 1) * width, :].rearrange("p (c n) i -> p c i n", n=PACK),
+                    in_=piece[:].rearrange("p i (c n) -> p c i n", n=PACK),
+                )
             nc.vector.quantize_mx(
                 out=codes[:].bitcast(FP8X4), scales=plane[:], in_=grouped[:].rearrange("p n i -> p (n i)")
             )
@@ -133,7 +138,7 @@ def tile_list_rgg_ownL_kernel(
                 out=bank[:],
                 lhsT=weight[0][:, b * width : (b + 1) * width].bitcast(weight[2]),
                 lhsT_scale=weight[1][:, b * P : (b + 1) * P],
-                rhs=words[:, cols].bitcast(FP8X4),
+                rhs=words[h].bitcast(FP8X4),
                 rhs_scale=plane[:, cols],
                 start=start,
                 stop=stop,
@@ -203,11 +208,10 @@ def tile_list_rgg_ownL_kernel(
         def store(b):
             rows = slice(b * P, (b + 1) * P)
             tile = out_rows[b % OUT_TILES]
-            if b < ROW_BLOCKS - 1:
-                nc.sync.dma_start(out=out[rows, :], in_=tile[:])
-            else:
-                nc.sync.dma_start(out=out[rows, 0 : T // 2], in_=tile[:, 0 : T // 2])
-                nc.scalar.dma_start(out=out[rows, T // 2 : T], in_=tile[:, T // 2 : T])
+            width = T // STORE_PIECES[b]
+            for i in range(STORE_PIECES[b]):
+                queue = nc.scalar if b == ROW_BLOCKS - 1 and i % 2 == 0 else nc.sync
+                queue.dma_start(out=out[rows, i * width : (i + 1) * width], in_=tile[:, i * width : (i + 1) * width])
 
 
         units = [(b, h) for b in range(ROW_BLOCKS) for h in range(HALVES)]

@@ -54,7 +54,7 @@ def tile_list_rgg_ownL_kernel(
         wb_s = keep.tile([P, N // 4], I32, name="wb_s", align_bytes=64)
         wc_w = keep.tile([P, N], I32, name="wc_w", align_bytes=64)
         wc_s = keep.tile([P, N // 4], I32, name="wc_s", align_bytes=64)
-        wa_raw = [keep.tile([P, PACK, N // 2], F32, name=f"wa_raw{i}", tag=f"wa_raw{i}", align_bytes=64) for i in range(2)]
+        wa_raw = keep.tile([P, PACK, N], F32, name="wa_raw")
         wo_raw = keep.tile([P, PACK, N], F32, name="wo_raw")
         wgo_rows = keep.tile([P, P], F32, name="wgo_rows")
         wgo_cols = keep.tile([P, EDGE_TILES], F32, name="wgo_cols")
@@ -73,15 +73,13 @@ def tile_list_rgg_ownL_kernel(
         nc.vector.memset(warm[:], 0.0)
         for tile in out_rows:
             nc.vector.memset(tile[:].bitcast(I32), 0)
-        nc.sync.dma_start(dst_list[:], offs2)
+        nc.sync.dma_start(src_list[:], offs)
         for q in (0, 2, 1, 3):
             load_scale_quadrant(nc.sync, tab_s, tab_scales, q)
         nc.scalar.activation(warmed[:], warm[:], SIGMOID)
-        nc.sync.dma_start(src_list[:], offs)
-        wa_rows = wa.rearrange("(p i) n -> p i n", i=PACK)
-        nc.sync.dma_start(out=wa_raw[0][:], in_=wa_rows[:, :, 0 : N // 2])
+        nc.sync.dma_start(dst_list[:], offs2)
         nc.sync.dma_start(out=tab_w[:], in_=tab_words[0].rearrange("p t i -> p (t i)").bitcast(I32))
-        nc.sync.dma_start(out=wa_raw[1][:], in_=wa_rows[:, :, N // 2 : N])
+        nc.sync.dma_start(out=wa_raw[:], in_=wa.rearrange("(p i) n -> p i n", i=PACK))
         for q in range(4):
             load_scale_quadrant(nc.sync, wc_s, wc_scales, q)
         nc.sync.dma_start(out=wo_raw[:], in_=wo.rearrange("(p i) n -> p i n", i=PACK))
@@ -94,28 +92,22 @@ def tile_list_rgg_ownL_kernel(
 
         src_s = keep.tile([P, J], U8, name="src_s", align_bytes=64)
         dst_s = keep.tile([P, J], U8, name="dst_s", align_bytes=64)
-        nc.vector.tensor_copy(dst_s[:], tab_s[:].bitcast(U8).indirect(dst_list[:]))
         nc.vector.tensor_copy(src_s[:], tab_s[:].bitcast(U8).indirect(src_list[:]))
+        nc.vector.tensor_copy(dst_s[:], tab_s[:].bitcast(U8).indirect(dst_list[:]))
+        src_w = keep.tile([P, J], U32, name="src_w", align_bytes=64)
+        dst_w = keep.tile([P, J], U32, name="dst_w", align_bytes=64)
+        nc.vector.tensor_copy(src_w[:], tab_w[:].bitcast(U32).indirect(src_list[:]))
+        nc.vector.tensor_copy(dst_w[:], tab_w[:].bitcast(U32).indirect(dst_list[:]))
 
-        def half_list(lst, h):
-            return lst[:, h * LIST_COLS_PER_HALF : (h + 1) * LIST_COLS_PER_HALF]
-
-        quantised, dst_w, src_w = [], [], []
-        for h, (label, raw) in enumerate((("wa", wa_raw), ("wo", [wo_raw]))):
-            both = keep.tile([P, 2 * BANK], U32, name="both", tag=("first_words", "wa_raw1")[h], align_bytes=64)
-            dst_w.append(both[:, 0:BANK])
-            src_w.append(both[:, BANK : 2 * BANK])
-            nc.vector.tensor_copy(dst_w[h], tab_w[:].bitcast(U32).indirect(half_list(dst_list, h)))
-            nc.vector.tensor_copy(src_w[h], tab_w[:].bitcast(U32).indirect(half_list(src_list, h)))
+        quantised = []
+        for label, raw in (("wa", wa_raw), ("wo", wo_raw)):
             grouped = keep.tile([P, N, PACK], BF16, name="grouped", tag=f"{label}_grouped", align_bytes=64)
             codes = keep.tile([P, N], U32, name=f"{label}_codes", align_bytes=64)
             plane = keep.tile([P, N], U8, name=f"{label}_plane", align_bytes=64)
-            width = N // len(raw)
-            for i, piece in enumerate(raw):
-                nc.scalar.copy(
-                    out=grouped[:, i * width : (i + 1) * width, :].rearrange("p (c n) i -> p c i n", n=PACK),
-                    in_=piece[:].rearrange("p i (c n) -> p c i n", n=PACK),
-                )
+            nc.scalar.copy(
+                out=grouped[:].rearrange("p (c n) i -> p c i n", n=PACK),
+                in_=raw[:].rearrange("p i (c n) -> p c i n", n=PACK),
+            )
             nc.vector.quantize_mx(
                 out=codes[:].bitcast(FP8X4), scales=plane[:], in_=grouped[:].rearrange("p n i -> p (n i)")
             )
@@ -138,7 +130,7 @@ def tile_list_rgg_ownL_kernel(
                 out=bank[:],
                 lhsT=weight[0][:, b * width : (b + 1) * width].bitcast(weight[2]),
                 lhsT_scale=weight[1][:, b * P : (b + 1) * P],
-                rhs=words[h].bitcast(FP8X4),
+                rhs=words[:, cols].bitcast(FP8X4),
                 rhs_scale=plane[:, cols],
                 start=start,
                 stop=stop,
@@ -148,11 +140,11 @@ def tile_list_rgg_ownL_kernel(
             return [(0, 1), (2, 3)] if (b, h) == (0, 0) else [(0, 1, 2, 3)]
 
         def unit(b, h):
-            za = psum.tile([P, BANK], F32, name="za")
-            mx_pass(za, wa_mx, P, b, dst_w, dst_s, h, True, False)
-            mx_pass(za, wb_mx, 2 * P, b, src_w, src_s, h, False, True)
             ms = psum.tile([P, BANK], F32, name="ms")
             mx_pass(ms, wc_mx, P, b, src_w, src_s, h, True, True)
+            za = psum.tile([P, BANK], F32, name="za")
+            mx_pass(za, wb_mx, 2 * P, b, src_w, src_s, h, True, False)
+            mx_pass(za, wa_mx, P, b, dst_w, dst_s, h, False, True)
             ow = psum.tile([P, BANK], F32, name="ow")
             mx_pass(ow, wo_mx, P, b, dst_w, dst_s, h, True, True)
             eta = ring.tile([P, BANK], F32, name="eta")
@@ -161,25 +153,30 @@ def tile_list_rgg_ownL_kernel(
                 message = keep.tile([P, BANK], F32, name="first_message", tag="wo_grouped", align_bytes=64)
             else:
                 message = ring.tile([P, BANK], F32, name="message")
+            nc.scalar.copy(out=source[:], in_=ms[:])
             for part in parts(b, h):
                 cols = slice(part[0] * P, (part[-1] + 1) * P)
                 nc.scalar.activation(eta[:, cols], za[:, cols], SIGMOID)
-                nc.scalar.copy(out=source[:, cols], in_=ms[:, cols])
                 nc.gpsimd.tensor_tensor(message[:, cols], source[:, cols], eta[:, cols], MULT)
             own = ring.tile([P, BANK], F32, name="own")
             nc.scalar.copy(out=own[:], in_=ow[:])
             return message, own
 
         def finish(b, h, message, own):
-            terms = (message, own, picked[b][:, h * BANK : (h + 1) * BANK])
+            terms = (own, picked[b][:, h * BANK : (h + 1) * BANK], message)
             weighted = ring.tile([P, BANK], F32, name="weighted")
             for part in parts(b, h):
                 total = psum.tile([P, BANK], F32, name="total", bufs=3)
-                for q in part:
-                    cols = slice(q * P, (q + 1) * P)
-                    for i, term in enumerate(terms):
+                for i, term in enumerate(terms):
+                    for q in part:
+                        cols = slice(q * P, (q + 1) * P)
                         nc.tensor.matmul(
-                            total[:, cols], term[:, cols], ident[:], start=(i == 0), stop=(i == len(terms) - 1), is_transpose=True
+                            total[:, cols],
+                            term[:, cols],
+                            ident[:],
+                            start=(i == 0 and q == part[0]),
+                            stop=(i == len(terms) - 1 and q == part[-1]),
+                            is_transpose=True,
                         )
                 for q in part:
                     cols = slice(q * P, (q + 1) * P)
@@ -199,11 +196,7 @@ def tile_list_rgg_ownL_kernel(
             elif h == HALVES - 1:
                 nc.vector.tensor_copy(window.indirect(dst_list[:]), result[b][:])
 
-        for b in range(1):
-            for h in range(HALVES):
-                cols = slice(h * BANK, (h + 1) * BANK)
-                nc.vector.tensor_copy(picked[b][:, cols], r_rows[b][:].indirect(half_list(dst_list, h)))
-        for b in range(1, ROW_BLOCKS):
+        for b in range(ROW_BLOCKS):
             nc.vector.tensor_copy(picked[b][:], r_rows[b][:].indirect(dst_list[:]))
         def store(b):
             rows = slice(b * P, (b + 1) * P)

@@ -49,30 +49,28 @@ def tile_list_rgg_ownL_kernel(
         src_list = keep.tile([P, J // 16], U16, name="src_list")
         dst_list = keep.tile([P, J // 16], U16, name="dst_list")
         tab_w = keep.tile([P, T], I32, name="tab_w", align_bytes=64)
-        tab_s = keep.tile([P, T // 4], I32, name="tab_s", align_bytes=64)
+        tab_s = keep.tile([P, T // 4], I32, name="tab_s", tag="tab_s", align_bytes=64)
         wb_w = keep.tile([P, N // 2], I32, name="wb_w", align_bytes=64)
         wb_s = keep.tile([P, N // 4], I32, name="wb_s", align_bytes=64)
         wc_w = keep.tile([P, N], I32, name="wc_w", align_bytes=64)
         wc_s = keep.tile([P, N // 4], I32, name="wc_s", align_bytes=64)
-        wa_raw = keep.tile([P, PACK, N], F32, name="wa_raw")
+        wa_raw = keep.tile([P, PACK, N], F32, name="wa_raw", tag="wa_raw")
         wo_raw = keep.tile([P, PACK, N], F32, name="wo_raw")
-        wgo_rows = keep.tile([P, P], F32, name="wgo_rows")
         wgo_cols = keep.tile([P, EDGE_TILES], F32, name="wgo_cols")
-        ident = keep.tile([P, P], F32, name="ident")
         r_rows = [keep.tile([P, T], F32, name=f"r_rows{b}", tag=f"r_rows{b}") for b in range(ROW_BLOCKS)]
-        out_rows = [keep.tile([P, T], F32, name=f"out_rows{i}") for i in range(OUT_TILES)]
+        out_rows = [keep.tile([P, T], F32, name="out_rows0")]
 
-        for plane in (tab_s, wc_s, wb_s):
-            nc.gpsimd.memset(plane[:], 0)
-        for q in range(4):
-            load_scale_quadrant(nc.gpsimd, wb_s, wb_scales, q)
-        make_identity(nc, ident[:])
-        nc.gpsimd.memset(wgo_rows[:], 0.0)
         warm = keep.tile([P, 1], F32, name="warm")
         warmed = keep.tile([P, 1], F32, name="warmed")
+        nc.vector.memset(tab_s[:], 0)
         nc.vector.memset(warm[:], 0.0)
-        for tile in out_rows:
-            nc.vector.memset(tile[:].bitcast(I32), 0)
+        for plane in (wb_s, wc_s):
+            nc.vector.memset(plane[:], 0)
+        wgo_rows = keep.tile([P, P], F32, name="wgo_rows")[:]
+        nc.vector.memset(wgo_rows, 0.0)
+        nc.vector.memset(out_rows[0][:].bitcast(I32), 0)
+        for q in range(4):
+            load_scale_quadrant(nc.gpsimd, wb_s, wb_scales, q)
         nc.sync.dma_start(src_list[:], offs)
         for q in (0, 2, 1, 3):
             load_scale_quadrant(nc.sync, tab_s, tab_scales, q)
@@ -85,15 +83,17 @@ def tile_list_rgg_ownL_kernel(
         nc.sync.dma_start(out=wo_raw[:], in_=wo.rearrange("(p i) n -> p i n", i=PACK))
         nc.sync.dma_start(out=wc_w[:], in_=wc_words[0].rearrange("p n i -> p (n i)").bitcast(I32))
         nc.sync.dma_start(out=wb_w[:], in_=wb_words[0].bitcast(I32))
-        for b in range(ROW_BLOCKS):
-            if b == 2:
-                nc.sync.dma_start(out=wgo_rows[0:EDGE_TILES, :], in_=wgo[0].rearrange("(e p) -> e p", p=P))
-            nc.sync.dma_start(out=r_rows[b][:], in_=rT[b * P : (b + 1) * P, :])
 
         src_s = keep.tile([P, J], U8, name="src_s", align_bytes=64)
         dst_s = keep.tile([P, J], U8, name="dst_s", align_bytes=64)
         nc.vector.tensor_copy(src_s[:], tab_s[:].bitcast(U8).indirect(src_list[:]))
         nc.vector.tensor_copy(dst_s[:], tab_s[:].bitcast(U8).indirect(dst_list[:]))
+        ident = keep.tile([P, P], F32, name="ident", tag="tab_s", align_bytes=64)[:]
+        make_identity(nc, ident)
+        for b in range(ROW_BLOCKS):
+            if b == 2:
+                nc.sync.dma_start(out=wgo_rows[0:EDGE_TILES, :], in_=wgo[0].rearrange("(e p) -> e p", p=P))
+            nc.sync.dma_start(out=r_rows[b][:], in_=rT[b * P : (b + 1) * P, :])
         src_w = keep.tile([P, J], U32, name="src_w", align_bytes=64)
         dst_w = keep.tile([P, J], U32, name="dst_w", align_bytes=64)
         nc.vector.tensor_copy(src_w[:], tab_w[:].bitcast(U32).indirect(src_list[:]))
@@ -112,12 +112,15 @@ def tile_list_rgg_ownL_kernel(
                 out=codes[:].bitcast(FP8X4), scales=plane[:], in_=grouped[:].rearrange("p n i -> p (n i)")
             )
             quantised.append((codes[:], plane[:], FP8X4))
+        second = keep.tile([P, T], F32, name="out_rows1", tag="wa_raw")
+        nc.gpsimd.memset(second[:].bitcast(I32), 0)
+        out_rows.append(second)
         wa_mx, wo_mx = quantised
         wb_mx = (wb_w[:].bitcast(U8), wb_s[:].bitcast(U8), FP4X4)
         wc_mx = (wc_w[:], wc_s[:].bitcast(U8), FP8X4)
 
         wgo_bank = psum.tile([P, BANK], F32, name="back", bufs=2)
-        nc.tensor.transpose(wgo_bank[:, 0:P], wgo_rows[:], ident[:])
+        nc.tensor.transpose(wgo_bank[:, 0:P], wgo_rows, ident)
         nc.scalar.copy(out=wgo_cols[:], in_=wgo_bank[:, 0:EDGE_TILES])
 
         picked = [keep.tile([P, J], F32, name=f"picked{b}") for b in range(ROW_BLOCKS)]
@@ -142,7 +145,7 @@ def tile_list_rgg_ownL_kernel(
         def unit(b, h):
             ms = psum.tile([P, BANK], F32, name="ms")
             mx_pass(ms, wc_mx, P, b, src_w, src_s, h, True, True)
-            za = psum.tile([P, BANK], F32, name="za")
+            za = psum.tile([P, BANK], F32, name="za", bufs=2)
             mx_pass(za, wb_mx, 2 * P, b, src_w, src_s, h, True, False)
             mx_pass(za, wa_mx, P, b, dst_w, dst_s, h, False, True)
             ow = psum.tile([P, BANK], F32, name="ow")
@@ -166,14 +169,14 @@ def tile_list_rgg_ownL_kernel(
             terms = (own, picked[b][:, h * BANK : (h + 1) * BANK], message)
             weighted = ring.tile([P, BANK], F32, name="weighted")
             for part in parts(b, h):
-                total = psum.tile([P, BANK], F32, name="total", bufs=3)
+                total = psum.tile([P, BANK], F32, name="total", bufs=2)
                 for i, term in enumerate(terms):
                     for q in part:
                         cols = slice(q * P, (q + 1) * P)
                         nc.tensor.matmul(
                             total[:, cols],
                             term[:, cols],
-                            ident[:],
+                            ident,
                             start=(i == 0 and q == part[0]),
                             stop=(i == len(terms) - 1 and q == part[-1]),
                             is_transpose=True,
@@ -185,7 +188,7 @@ def tile_list_rgg_ownL_kernel(
                 back = psum.tile([P, BANK], F32, name="back", bufs=2)
                 for q in part:
                     cols = slice(q * P, (q + 1) * P)
-                    nc.tensor.transpose(back[:, cols], weighted[:, cols], ident[:])
+                    nc.tensor.transpose(back[:, cols], weighted[:, cols], ident)
                 first, last = part[0] * P, (part[-1] + 1) * P
                 nc.scalar.copy(out=result[b][:, h * BANK + first : h * BANK + last], in_=back[:, first:last])
             cols = slice(h * BANK, (h + 1) * BANK)

@@ -68,6 +68,9 @@ def tile_list_rgg_ownL_kernel(
             nc.vector.memset(plane[:], 0)
         wgo_rows = keep.tile([P, P], F32, name="wgo_rows")[:]
         nc.vector.memset(wgo_rows, 0.0)
+        ident = keep.tile([P, P], F32, name="ident")[:]
+        nc.vector.memset(ident, 0.0)
+        make_identity(nc, ident, nomemset=True)
         nc.vector.memset(out_rows[0][:].bitcast(I32), 0)
         for q in range(4):
             load_scale_quadrant(nc.gpsimd, wb_s, wb_scales, q)
@@ -88,8 +91,9 @@ def tile_list_rgg_ownL_kernel(
         dst_s = keep.tile([P, J], U8, name="dst_s", align_bytes=64)
         nc.vector.tensor_copy(src_s[:], tab_s[:].bitcast(U8).indirect(src_list[:]))
         nc.vector.tensor_copy(dst_s[:], tab_s[:].bitcast(U8).indirect(dst_list[:]))
-        ident = keep.tile([P, P], F32, name="ident", tag="tab_s", align_bytes=64)[:]
-        make_identity(nc, ident)
+        second = keep.tile([P, T], F32, name="out_rows1", tag="tab_s", align_bytes=64)
+        nc.gpsimd.memset(second[:].bitcast(I32), 0)
+        out_rows.append(second)
         for b in range(ROW_BLOCKS):
             if b == 2:
                 nc.sync.dma_start(out=wgo_rows[0:EDGE_TILES, :], in_=wgo[0].rearrange("(e p) -> e p", p=P))
@@ -112,9 +116,6 @@ def tile_list_rgg_ownL_kernel(
                 out=codes[:].bitcast(FP8X4), scales=plane[:], in_=grouped[:].rearrange("p n i -> p (n i)")
             )
             quantised.append((codes[:], plane[:], FP8X4))
-        second = keep.tile([P, T], F32, name="out_rows1", tag="wa_raw")
-        nc.gpsimd.memset(second[:].bitcast(I32), 0)
-        out_rows.append(second)
         wa_mx, wo_mx = quantised
         wb_mx = (wb_w[:].bitcast(U8), wb_s[:].bitcast(U8), FP4X4)
         wc_mx = (wc_w[:], wc_s[:].bitcast(U8), FP8X4)

@@ -26,7 +26,7 @@ ROW_BLOCKS = N // P
 HALVES = J // BANK
 TILES_PER_HALF = BANK // P
 LIST_COLS_PER_HALF = BANK // 16
-OUT_TILES = 2
+OUT_TILES = 3
 AHEAD = 2
 STORE_PIECES = (1, 2, 4, 4)
 FIRST_PART = 2 * P
@@ -152,7 +152,10 @@ def tile_list_rgg_ownL_kernel(
             ow = psum.tile([P, BANK], F32, name="ow")
             mx_pass(ow, wo_mx, P, b, dst_w, dst_s, h, True, True)
             eta = ring.tile([P, BANK], F32, name="eta")
-            source = ring.tile([P, BANK], F32, name="source")
+            if (b, h) == (1, 1):
+                source = keep.tile([P, BANK], F32, name="fourth_source", tag="third_out")
+            else:
+                source = ring.tile([P, BANK], F32, name="source")
             if (b, h) == (0, 0):
                 message = keep.tile([P, BANK], F32, name="first_message", tag="wo_grouped", align_bytes=64)
             else:
@@ -162,6 +165,10 @@ def tile_list_rgg_ownL_kernel(
                 cols = slice(part[0] * P, (part[-1] + 1) * P)
                 nc.scalar.activation(eta[:, cols], za[:, cols], SIGMOID)
                 nc.gpsimd.tensor_tensor(message[:, cols], source[:, cols], eta[:, cols], MULT)
+            if (b, h) == (1, 1):
+                third = keep.tile([P, T], F32, name="out_rows2", tag="third_out")
+                nc.gpsimd.memset(third[:].bitcast(I32), 0)
+                out_rows.append(third)
             own = ring.tile([P, BANK], F32, name="own")
             nc.scalar.copy(out=own[:], in_=ow[:])
             return message, own
@@ -194,8 +201,9 @@ def tile_list_rgg_ownL_kernel(
                 nc.scalar.copy(out=result[b][:, h * BANK + first : h * BANK + last], in_=back[:, first:last])
             cols = slice(h * BANK, (h + 1) * BANK)
             window = out_rows[b % OUT_TILES][:]
-            if b < 1:
-                first, last = (0, FIRST_PART) if h == 0 else (FIRST_PART, J)
+            if b < 2:
+                cut = (FIRST_PART, BANK)[b]
+                first, last = (0, cut) if h == 0 else (cut, J)
                 nc.vector.tensor_copy(window.indirect(dst_list[:, first // 16 : last // 16]), result[b][:, first:last])
             elif h == HALVES - 1:
                 nc.vector.tensor_copy(window.indirect(dst_list[:]), result[b][:])
@@ -211,7 +219,7 @@ def tile_list_rgg_ownL_kernel(
                 queue.dma_start(out=out[rows, i * width : (i + 1) * width], in_=tile[:, i * width : (i + 1) * width])
 
 
-        units = [(b, h) for b in range(ROW_BLOCKS) for h in range(HALVES)]
+        units = [(b, h) for h in range(HALVES) for b in range(2)] + [(b, h) for b in range(2, ROW_BLOCKS) for h in range(HALVES)]
         staged = [unit(b, h) for b, h in units[:AHEAD]]
         for u, (b, h) in enumerate(units):
             finish(b, h, *staged[u])

@@ -58,20 +58,19 @@ def tile_list_rgg_ownL_kernel(
         wo_raw = keep.tile([P, PACK, N], F32, name="wo_raw")
         wgo_cols = keep.tile([P, EDGE_TILES], F32, name="wgo_cols")
         r_rows = [keep.tile([P, T], F32, name=f"r_rows{b}", tag=f"r_rows{b}") for b in range(ROW_BLOCKS)]
-        out_rows = [keep.tile([P, T], F32, name="out_rows0")]
+        out_rows = []
 
         warm = keep.tile([P, 1], F32, name="warm")
         warmed = keep.tile([P, 1], F32, name="warmed")
         nc.vector.memset(tab_s[:], 0)
         nc.vector.memset(warm[:], 0.0)
-        for plane in (wb_s, wc_s):
-            nc.vector.memset(plane[:], 0)
+        nc.vector.memset(wc_s[:], 0)
         wgo_rows = keep.tile([P, P], F32, name="wgo_rows")[:]
         nc.vector.memset(wgo_rows, 0.0)
         ident = keep.tile([P, P], F32, name="ident")[:]
         nc.vector.memset(ident, 0.0)
         make_identity(nc, ident, nomemset=True)
-        nc.vector.memset(out_rows[0][:].bitcast(I32), 0)
+        nc.vector.memset(wb_s[:], 0)
         for q in range(4):
             load_scale_quadrant(nc.gpsimd, wb_s, wb_scales, q)
         nc.sync.dma_start(src_list[:], offs)
@@ -152,8 +151,8 @@ def tile_list_rgg_ownL_kernel(
             ow = psum.tile([P, BANK], F32, name="ow")
             mx_pass(ow, wo_mx, P, b, dst_w, dst_s, h, True, True)
             eta = ring.tile([P, BANK], F32, name="eta")
-            if (b, h) == (1, 1):
-                source = keep.tile([P, BANK], F32, name="fourth_source", tag="third_out")
+            if b == 1:
+                source = keep.tile([P, BANK], F32, name="held_source", tag=f"late_out{h}")
             else:
                 source = ring.tile([P, BANK], F32, name="source")
             if (b, h) == (0, 0):
@@ -165,8 +164,8 @@ def tile_list_rgg_ownL_kernel(
                 cols = slice(part[0] * P, (part[-1] + 1) * P)
                 nc.scalar.activation(eta[:, cols], za[:, cols], SIGMOID)
                 nc.gpsimd.tensor_tensor(message[:, cols], source[:, cols], eta[:, cols], MULT)
-            if (b, h) == (1, 1):
-                third = keep.tile([P, T], F32, name="out_rows2", tag="third_out")
+            if b == 1:
+                third = keep.tile([P, T], F32, name="late_out", tag=f"late_out{h}")
                 nc.gpsimd.memset(third[:].bitcast(I32), 0)
                 out_rows.append(third)
             own = ring.tile([P, BANK], F32, name="own")

@@ -54,23 +54,27 @@ def tile_list_rgg_ownL_kernel(
         wb_s = keep.tile([P, N // 4], I32, name="wb_s", align_bytes=64)
         wc_w = keep.tile([P, N], I32, name="wc_w", align_bytes=64)
         wc_s = keep.tile([P, N // 4], I32, name="wc_s", align_bytes=64)
-        wa_raw = keep.tile([P, PACK, N], F32, name="wa_raw", tag="wa_raw")
+        wa_raw = keep.tile([P, PACK, N], F32, name="wa_raw", tag="wa_raw", align_bytes=64)
         wo_raw = keep.tile([P, PACK, N], F32, name="wo_raw")
-        wgo_cols = keep.tile([P, EDGE_TILES], F32, name="wgo_cols")
+        wgo_cols = [keep.tile([P, TILES_PER_HALF], F32, name=f"wgo_cols{h}") for h in range(HALVES)]
         r_rows = [keep.tile([P, T], F32, name=f"r_rows{b}", tag=f"r_rows{b}") for b in range(ROW_BLOCKS)]
-        out_rows = []
+        out_rows = {}
 
         warm = keep.tile([P, 1], F32, name="warm")
         warmed = keep.tile([P, 1], F32, name="warmed")
         nc.vector.memset(tab_s[:], 0)
         nc.vector.memset(warm[:], 0.0)
         nc.vector.memset(wc_s[:], 0)
-        wgo_rows = keep.tile([P, P], F32, name="wgo_rows")[:]
-        nc.vector.memset(wgo_rows, 0.0)
+        wgo_rows = [keep.tile([P, P], F32, name=f"wgo_rows{h}", tag=f"wgo_rows{h}", align_bytes=64)[:] for h in range(HALVES)]
+        wgo_late = keep.tile([P, P], F32, name="wgo_late", tag="wgo_late", align_bytes=64)[:]
+        for rows in wgo_rows:
+            nc.vector.memset(rows, 0.0)
         ident = keep.tile([P, P], F32, name="ident")[:]
         nc.vector.memset(ident, 0.0)
         make_identity(nc, ident, nomemset=True)
         nc.vector.memset(wb_s[:], 0)
+        out_rows[0] = keep.tile([P, T], F32, name="first_out")
+        nc.vector.memset(out_rows[0][:].bitcast(I32), 0)
         for q in range(4):
             load_scale_quadrant(nc.gpsimd, wb_s, wb_scales, q)
         nc.sync.dma_start(src_list[:], offs)
@@ -92,18 +96,24 @@ def tile_list_rgg_ownL_kernel(
         nc.vector.tensor_copy(dst_s[:], tab_s[:].bitcast(U8).indirect(dst_list[:]))
         second = keep.tile([P, T], F32, name="out_rows1", tag="tab_s", align_bytes=64)
         nc.gpsimd.memset(second[:].bitcast(I32), 0)
-        out_rows.append(second)
+        out_rows[1] = second
         for b in range(ROW_BLOCKS):
-            if b == 2:
-                nc.sync.dma_start(out=wgo_rows[0:EDGE_TILES, :], in_=wgo[0].rearrange("(e p) -> e p", p=P))
+            if b == 1:
+                nc.sync.dma_start(out=wgo_rows[0][0:TILES_PER_HALF, :], in_=wgo[0, 0:BANK].rearrange("(e p) -> e p", p=P))
+            if b == 3:
+                nc.sync.dma_start(out=wgo_late[0:TILES_PER_HALF, :], in_=wgo[0, BANK:J].rearrange("(e p) -> e p", p=P))
             nc.sync.dma_start(out=r_rows[b][:], in_=rT[b * P : (b + 1) * P, :])
-        src_w = keep.tile([P, J], U32, name="src_w", align_bytes=64)
-        dst_w = keep.tile([P, J], U32, name="dst_w", align_bytes=64)
-        nc.vector.tensor_copy(src_w[:], tab_w[:].bitcast(U32).indirect(src_list[:]))
-        nc.vector.tensor_copy(dst_w[:], tab_w[:].bitcast(U32).indirect(dst_list[:]))
 
-        quantised = []
-        for label, raw in (("wa", wa_raw), ("wo", wo_raw)):
+        def half_list(lst, h):
+            return lst[:, h * LIST_COLS_PER_HALF : (h + 1) * LIST_COLS_PER_HALF]
+
+        quantised, src_w, dst_w = [], [], []
+        for h, (label, raw) in enumerate((("wa", wa_raw), ("wo", wo_raw))):
+            both = keep.tile([P, 2 * BANK], U32, name="both", tag=("first_words", "wa_raw")[h], align_bytes=64)
+            src_w.append(both[:, 0:BANK])
+            dst_w.append(both[:, BANK : 2 * BANK])
+            nc.vector.tensor_copy(src_w[h], tab_w[:].bitcast(U32).indirect(half_list(src_list, h)))
+            nc.vector.tensor_copy(dst_w[h], tab_w[:].bitcast(U32).indirect(half_list(dst_list, h)))
             grouped = keep.tile([P, N, PACK], BF16, name="grouped", tag=f"{label}_grouped", align_bytes=64)
             codes = keep.tile([P, N], U32, name=f"{label}_codes", align_bytes=64)
             plane = keep.tile([P, N], U8, name=f"{label}_plane", align_bytes=64)
@@ -119,9 +129,6 @@ def tile_list_rgg_ownL_kernel(
         wb_mx = (wb_w[:].bitcast(U8), wb_s[:].bitcast(U8), FP4X4)
         wc_mx = (wc_w[:], wc_s[:].bitcast(U8), FP8X4)
 
-        wgo_bank = psum.tile([P, BANK], F32, name="back", bufs=2)
-        nc.tensor.transpose(wgo_bank[:, 0:P], wgo_rows, ident)
-        nc.scalar.copy(out=wgo_cols[:], in_=wgo_bank[:, 0:EDGE_TILES])
 
         picked = [keep.tile([P, J], F32, name=f"picked{b}") for b in range(ROW_BLOCKS)]
 
@@ -133,7 +140,7 @@ def tile_list_rgg_ownL_kernel(
                 out=bank[:],
                 lhsT=weight[0][:, b * width : (b + 1) * width].bitcast(weight[2]),
                 lhsT_scale=weight[1][:, b * P : (b + 1) * P],
-                rhs=words[:, cols].bitcast(FP8X4),
+                rhs=words[h].bitcast(FP8X4),
                 rhs_scale=plane[:, cols],
                 start=start,
                 stop=stop,
@@ -143,20 +150,26 @@ def tile_list_rgg_ownL_kernel(
             return [(0, 1), (2, 3)] if (b, h) == (0, 0) else [(0, 1, 2, 3)]
 
         def unit(b, h):
-            ms = psum.tile([P, BANK], F32, name="ms")
+            u = units.index((b, h))
+            ms = psum.tile([P, BANK], F32, name="ms", tag=f"back{u % 2}" if u in (2, 3) else "ms")
             mx_pass(ms, wc_mx, P, b, src_w, src_s, h, True, True)
             za = psum.tile([P, BANK], F32, name="za", bufs=2)
             mx_pass(za, wb_mx, 2 * P, b, src_w, src_s, h, True, False)
             mx_pass(za, wa_mx, P, b, dst_w, dst_s, h, False, True)
             ow = psum.tile([P, BANK], F32, name="ow")
             mx_pass(ow, wo_mx, P, b, dst_w, dst_s, h, True, True)
-            eta = ring.tile([P, BANK], F32, name="eta")
-            if b == 1:
+            if b < 2 and h == 1:
+                eta = keep.tile([P, BANK], F32, name="held_eta", tag=("wo_grouped", "weighted1")[b], align_bytes=64)
+            else:
+                eta = ring.tile([P, BANK], F32, name="eta")
+            if (b, h) == (1, 1):
                 source = keep.tile([P, BANK], F32, name="held_source", tag=f"late_out{h}")
             else:
                 source = ring.tile([P, BANK], F32, name="source")
             if (b, h) == (0, 0):
                 message = keep.tile([P, BANK], F32, name="first_message", tag="wo_grouped", align_bytes=64)
+            elif (b, h) == (0, 1):
+                message = keep.tile([P, BANK], F32, name="third_message", tag="first_result")
             else:
                 message = ring.tile([P, BANK], F32, name="message")
             nc.scalar.copy(out=source[:], in_=ms[:])
@@ -164,17 +177,27 @@ def tile_list_rgg_ownL_kernel(
                 cols = slice(part[0] * P, (part[-1] + 1) * P)
                 nc.scalar.activation(eta[:, cols], za[:, cols], SIGMOID)
                 nc.gpsimd.tensor_tensor(message[:, cols], source[:, cols], eta[:, cols], MULT)
-            if b == 1:
+            if (b, h) == (1, 1):
                 third = keep.tile([P, T], F32, name="late_out", tag=f"late_out{h}")
                 nc.gpsimd.memset(third[:].bitcast(I32), 0)
-                out_rows.append(third)
-            own = ring.tile([P, BANK], F32, name="own")
-            nc.scalar.copy(out=own[:], in_=ow[:])
+                out_rows[2] = third
+            if (b, h) == (0, 1):
+                own = keep.tile([P, BANK], F32, name="held_own", tag="weighted0", align_bytes=64)
+            else:
+                own = ring.tile([P, BANK], F32, name="own")
+            for part in parts(b, h):
+                cols = slice(part[0] * P, (part[-1] + 1) * P)
+                nc.scalar.copy(out=own[:, cols], in_=ow[:, cols])
             return message, own
 
         def finish(b, h, message, own):
+            if (b, h) == (0, 0):
+                first_result = keep.tile([P, BANK], F32, name="first_result", tag="first_result")
             terms = (own, picked[b][:, h * BANK : (h + 1) * BANK], message)
-            weighted = ring.tile([P, BANK], F32, name="weighted")
+            if b < 2 and h == 0:
+                weighted = keep.tile([P, BANK], F32, name="first_weighted", tag=f"weighted{b}", align_bytes=64)
+            else:
+                weighted = ring.tile([P, BANK], F32, name="weighted")
             for part in parts(b, h):
                 total = psum.tile([P, BANK], F32, name="total", bufs=2)
                 for i, term in enumerate(terms):
@@ -190,24 +213,31 @@ def tile_list_rgg_ownL_kernel(
                         )
                 for q in part:
                     cols = slice(q * P, (q + 1) * P)
-                    e = h * TILES_PER_HALF + q
-                    nc.scalar.activation(weighted[:, cols], total[:, cols], COPY, scale=wgo_cols[:, e : e + 1])
-                back = psum.tile([P, BANK], F32, name="back", bufs=2)
+                    nc.scalar.activation(weighted[:, cols], total[:, cols], COPY, scale=wgo_cols[h][:, q : q + 1])
+                back = psum.tile([P, BANK], F32, name="back", tag=f"back{(units.index((b, h)) + part[0] // 2) % 2}")
                 for q in part:
                     cols = slice(q * P, (q + 1) * P)
                     nc.tensor.transpose(back[:, cols], weighted[:, cols], ident)
                 first, last = part[0] * P, (part[-1] + 1) * P
-                nc.scalar.copy(out=result[b][:, h * BANK + first : h * BANK + last], in_=back[:, first:last])
+                if (b, h) == (0, 0):
+                    nc.scalar.copy(out=first_result[:, first:last], in_=back[:, first:last])
+                else:
+                    nc.scalar.copy(out=result[b][:, h * BANK + first : h * BANK + last], in_=back[:, first:last])
             cols = slice(h * BANK, (h + 1) * BANK)
             window = out_rows[b % OUT_TILES][:]
-            if b < 2:
-                cut = (FIRST_PART, BANK)[b]
-                first, last = (0, cut) if h == 0 else (cut, J)
-                nc.vector.tensor_copy(window.indirect(dst_list[:, first // 16 : last // 16]), result[b][:, first:last])
+            if (b, h) == (0, 0):
+                values = keep.tile([P, BANK], F32, name="first_values", tag="wgo_late", align_bytes=64)
+                for first, last in ((0, FIRST_PART), (FIRST_PART, BANK)):
+                    nc.gpsimd.tensor_copy(values[:, first:last], first_result[:, first:last])
+                    nc.vector.tensor_copy(window.indirect(dst_list[:, first // 16 : last // 16]), values[:, first:last])
+            elif b < 2:
+                nc.vector.tensor_copy(window.indirect(half_list(dst_list, h)), result[b][:, cols])
             elif h == HALVES - 1:
                 nc.vector.tensor_copy(window.indirect(dst_list[:]), result[b][:])
 
-        for b in range(ROW_BLOCKS):
+        for first, last in ((0, FIRST_PART), (FIRST_PART, J)):
+            nc.vector.tensor_copy(picked[0][:, first:last], r_rows[0][:].indirect(dst_list[:, first // 16 : last // 16]))
+        for b in range(1, ROW_BLOCKS):
             nc.vector.tensor_copy(picked[b][:], r_rows[b][:].indirect(dst_list[:]))
         def store(b):
             rows = slice(b * P, (b + 1) * P)
@@ -220,7 +250,16 @@ def tile_list_rgg_ownL_kernel(
 
         units = [(b, h) for h in range(HALVES) for b in range(2)] + [(b, h) for b in range(2, ROW_BLOCKS) for h in range(HALVES)]
         staged = [unit(b, h) for b, h in units[:AHEAD]]
+        nc.gpsimd.tensor_copy(wgo_rows[1][0:TILES_PER_HALF, :], wgo_late[0:TILES_PER_HALF, :])
+
+        def turn_wgo(h, bank):
+            nc.tensor.transpose(bank[:, 0:P], wgo_rows[h], ident)
+            nc.scalar.copy(out=wgo_cols[h][:], in_=bank[:, 0:TILES_PER_HALF])
+
+        turn_wgo(0, psum.tile([P, BANK], F32, name="early_turn", tag="ms"))
         for u, (b, h) in enumerate(units):
+            if (b, h) == (0, 1):
+                turn_wgo(1, psum.tile([P, BANK], F32, name="late_turn", tag="ms"))
             finish(b, h, *staged[u])
             if h == HALVES - 1:
                 store(b)

@@ -21,20 +21,40 @@ SIGMOID = mybir.ActivationFunctionType.Sigmoid
 P = 128
 PACK = 4
 BANK = 512
-EDGE_TILES = J // P
-ROW_BLOCKS = N // P
+PER_COLUMN = 16
+SLABS = N // P
 HALVES = J // BANK
 TILES_PER_HALF = BANK // P
-LIST_COLS_PER_HALF = BANK // 16
+PAIRED = 2
 OUT_TILES = 3
 AHEAD = 2
+STAGE_BUFS = 4
+PART = 2 * P
+TAIL_SLAB = 2
+TAIL = J - PART
 STORE_PIECES = (1, 2, 4, 4)
-FIRST_PART = 2 * P
+
+UNITS = [(b, h) for h in range(HALVES) for b in range(PAIRED)] + [
+    (b, h) for b in range(PAIRED, SLABS) for h in range(HALVES)
+]
+FIRST, SECOND, THIRD, FOURTH = range(4)
 
 
 def load_scale_quadrant(queue, plane, scales, q):
     rows = scales[0].bitcast(I32)
     queue.dma_start(out=plane[32 * q : 32 * q + 4, :], in_=rows[4 * q : 4 * q + 4, :])
+
+
+def entries(lst, first, last):
+    return lst[:, first // PER_COLUMN : last // PER_COLUMN]
+
+
+def parts(u):
+    return [(0, 1), (2, 3)] if u == FIRST else [(0, 1, 2, 3)]
+
+
+def span(part):
+    return slice(part[0] * P, (part[-1] + 1) * P)
 
 
 def tile_list_rgg_ownL_kernel(
@@ -43,11 +63,11 @@ def tile_list_rgg_ownL_kernel(
     nc = tc.nc
     with ExitStack() as ctx:
         keep = ctx.enter_context(tc.tile_pool(name="keep", bufs=1))
-        ring = ctx.enter_context(tc.tile_pool(name="ring", bufs=4))
+        ring = ctx.enter_context(tc.tile_pool(name="ring", bufs=STAGE_BUFS))
         psum = ctx.enter_context(tc.psum_pool(name="psum", bufs=1))
 
-        src_list = keep.tile([P, J // 16], U16, name="src_list")
-        dst_list = keep.tile([P, J // 16], U16, name="dst_list")
+        src_list = keep.tile([P, J // PER_COLUMN], U16, name="src_list")
+        dst_list = keep.tile([P, J // PER_COLUMN], U16, name="dst_list")
         tab_w = keep.tile([P, T], I32, name="tab_w", align_bytes=64)
         tab_s = keep.tile([P, T // 4], I32, name="tab_s", tag="tab_s", align_bytes=64)
         wb_w = keep.tile([P, N // 2], I32, name="wb_w", align_bytes=64)
@@ -57,24 +77,25 @@ def tile_list_rgg_ownL_kernel(
         wa_raw = keep.tile([P, PACK, N], F32, name="wa_raw", tag="wa_raw", align_bytes=64)
         wo_raw = keep.tile([P, PACK, N], F32, name="wo_raw")
         wgo_cols = [keep.tile([P, TILES_PER_HALF], F32, name=f"wgo_cols{h}") for h in range(HALVES)]
-        r_rows = [keep.tile([P, T], F32, name=f"r_rows{b}", tag=f"r_rows{b}") for b in range(ROW_BLOCKS)]
-        out_rows = {}
-
+        r_rows = [keep.tile([P, T], F32, name=f"r_rows{b}") for b in range(SLABS)]
         warm = keep.tile([P, 1], F32, name="warm")
         warmed = keep.tile([P, 1], F32, name="warmed")
+        wgo_rows = [keep.tile([P, P], F32, name=f"wgo_rows{h}", align_bytes=64) for h in range(HALVES)]
+        wgo_late = keep.tile([P, P], F32, name="wgo_late", tag="wgo_late", align_bytes=64)
+        ident = keep.tile([P, P], F32, name="ident")
+        first_out = keep.tile([P, T], F32, name="first_out")
+        out_rows = [first_out]
+
         nc.vector.memset(tab_s[:], 0)
         nc.vector.memset(warm[:], 0.0)
         nc.vector.memset(wc_s[:], 0)
-        wgo_rows = [keep.tile([P, P], F32, name=f"wgo_rows{h}", tag=f"wgo_rows{h}", align_bytes=64)[:] for h in range(HALVES)]
-        wgo_late = keep.tile([P, P], F32, name="wgo_late", tag="wgo_late", align_bytes=64)[:]
         for rows in wgo_rows:
-            nc.vector.memset(rows, 0.0)
-        ident = keep.tile([P, P], F32, name="ident")[:]
-        nc.vector.memset(ident, 0.0)
-        make_identity(nc, ident, nomemset=True)
+            nc.vector.memset(rows[:], 0.0)
+        nc.vector.memset(ident[:], 0.0)
+        make_identity(nc, ident[:], nomemset=True)
         nc.vector.memset(wb_s[:], 0)
-        out_rows[0] = keep.tile([P, T], F32, name="first_out")
-        nc.vector.memset(out_rows[0][:].bitcast(I32), 0)
+        nc.vector.memset(first_out[:].bitcast(I32), 0)
+
         for q in range(4):
             load_scale_quadrant(nc.gpsimd, wb_s, wb_scales, q)
         nc.sync.dma_start(src_list[:], offs)
@@ -94,26 +115,24 @@ def tile_list_rgg_ownL_kernel(
         dst_s = keep.tile([P, J], U8, name="dst_s", align_bytes=64)
         nc.vector.tensor_copy(src_s[:], tab_s[:].bitcast(U8).indirect(src_list[:]))
         nc.vector.tensor_copy(dst_s[:], tab_s[:].bitcast(U8).indirect(dst_list[:]))
-        second = keep.tile([P, T], F32, name="out_rows1", tag="tab_s", align_bytes=64)
-        nc.gpsimd.memset(second[:].bitcast(I32), 0)
-        out_rows[1] = second
-        for b in range(ROW_BLOCKS):
+        second_out = keep.tile([P, T], F32, name="second_out", tag="tab_s", align_bytes=64)
+        nc.gpsimd.memset(second_out[:].bitcast(I32), 0)
+        out_rows.append(second_out)
+
+        for b in range(SLABS):
             if b == 1:
                 nc.sync.dma_start(out=wgo_rows[0][0:TILES_PER_HALF, :], in_=wgo[0, 0:BANK].rearrange("(e p) -> e p", p=P))
-            if b == 3:
+            if b == TAIL_SLAB + 1:
                 nc.sync.dma_start(out=wgo_late[0:TILES_PER_HALF, :], in_=wgo[0, BANK:J].rearrange("(e p) -> e p", p=P))
             nc.sync.dma_start(out=r_rows[b][:], in_=rT[b * P : (b + 1) * P, :])
 
-        def half_list(lst, h):
-            return lst[:, h * LIST_COLS_PER_HALF : (h + 1) * LIST_COLS_PER_HALF]
-
-        quantised, src_w, dst_w = [], [], []
+        src_all = keep.tile([P, J], U32, name="src_all", align_bytes=64)
+        nc.vector.tensor_copy(src_all[:], tab_w[:].bitcast(U32).indirect(src_list[:]))
+        src_w = [src_all[:, h * BANK : (h + 1) * BANK] for h in range(HALVES)]
+        quantised, dst_w = [], []
         for h, (label, raw) in enumerate((("wa", wa_raw), ("wo", wo_raw))):
-            both = keep.tile([P, 2 * BANK], U32, name="both", tag=("first_words", "wa_raw")[h], align_bytes=64)
-            src_w.append(both[:, 0:BANK])
-            dst_w.append(both[:, BANK : 2 * BANK])
-            nc.vector.tensor_copy(src_w[h], tab_w[:].bitcast(U32).indirect(half_list(src_list, h)))
-            nc.vector.tensor_copy(dst_w[h], tab_w[:].bitcast(U32).indirect(half_list(dst_list, h)))
+            dst_w.append(keep.tile([P, BANK], U32, name="dst_w", tag=("dst_first", "wa_raw")[h], align_bytes=64)[:])
+            nc.vector.tensor_copy(dst_w[h], tab_w[:].bitcast(U32).indirect(entries(dst_list, h * BANK, (h + 1) * BANK)))
             grouped = keep.tile([P, N, PACK], BF16, name="grouped", tag=f"{label}_grouped", align_bytes=64)
             codes = keep.tile([P, N], U32, name=f"{label}_codes", align_bytes=64)
             plane = keep.tile([P, N], U8, name=f"{label}_plane", align_bytes=64)
@@ -124,144 +143,137 @@ def tile_list_rgg_ownL_kernel(
             nc.vector.quantize_mx(
                 out=codes[:].bitcast(FP8X4), scales=plane[:], in_=grouped[:].rearrange("p n i -> p (n i)")
             )
-            quantised.append((codes[:], plane[:], FP8X4))
+            quantised.append((codes[:], plane[:], FP8X4, P))
         wa_mx, wo_mx = quantised
-        wb_mx = (wb_w[:].bitcast(U8), wb_s[:].bitcast(U8), FP4X4)
-        wc_mx = (wc_w[:], wc_s[:].bitcast(U8), FP8X4)
+        wb_mx = (wb_w[:].bitcast(U8), wb_s[:].bitcast(U8), FP4X4, 2 * P)
+        wc_mx = (wc_w[:], wc_s[:].bitcast(U8), FP8X4, P)
 
+        picked = [keep.tile([P, J], F32, name=f"picked{b}") for b in range(SLABS)]
+        result = [keep.tile([P, J], F32, name=f"result{b}") for b in range(SLABS)]
+        for first, last in ((0, PART), (PART, J)):
+            nc.vector.tensor_copy(picked[0][:, first:last], r_rows[0][:].indirect(entries(dst_list, first, last)))
+        for b in range(1, SLABS):
+            last = TAIL if b == TAIL_SLAB else J
+            nc.vector.tensor_copy(picked[b][:, 0:last], r_rows[b][:].indirect(entries(dst_list, 0, last)))
+        picked_tail = []
 
-        picked = [keep.tile([P, J], F32, name=f"picked{b}") for b in range(ROW_BLOCKS)]
+        def state(b, edge):
+            if b == TAIL_SLAB and edge >= TAIL:
+                return picked_tail[0][:, edge - TAIL : edge - TAIL + P]
+            return picked[b][:, edge : edge + P]
 
-        result = [keep.tile([P, J], F32, name=f"result{b}") for b in range(ROW_BLOCKS)]
-
-        def mx_pass(bank, weight, width, b, words, plane, h, start, stop):
-            cols = slice(h * BANK, (h + 1) * BANK)
+        def mx_pass(bank, weight, b, words, plane, h, start, stop):
+            w_words, w_plane, w_dtype, width = weight
             nc.tensor.matmul_mx(
                 out=bank[:],
-                lhsT=weight[0][:, b * width : (b + 1) * width].bitcast(weight[2]),
-                lhsT_scale=weight[1][:, b * P : (b + 1) * P],
+                lhsT=w_words[:, b * width : (b + 1) * width].bitcast(w_dtype),
+                lhsT_scale=w_plane[:, b * P : (b + 1) * P],
                 rhs=words[h].bitcast(FP8X4),
-                rhs_scale=plane[:, cols],
+                rhs_scale=plane[:, h * BANK : (h + 1) * BANK],
                 start=start,
                 stop=stop,
             )
 
-        def parts(b, h):
-            return [(0, 1), (2, 3)] if (b, h) == (0, 0) else [(0, 1, 2, 3)]
+        def stage_tile(name, u, takes_over, aligned):
+            if u not in takes_over:
+                return ring.tile([P, BANK], F32, name=name)
+            if aligned:
+                return keep.tile([P, BANK], F32, name=f"{name}{u}", tag=takes_over[u], align_bytes=64)
+            return keep.tile([P, BANK], F32, name=f"{name}{u}", tag=takes_over[u])
 
-        def unit(b, h):
-            u = units.index((b, h))
-            ms = psum.tile([P, BANK], F32, name="ms", tag=f"back{u % 2}" if u in (2, 3) else "ms")
-            mx_pass(ms, wc_mx, P, b, src_w, src_s, h, True, True)
+        def products(u):
+            b, h = UNITS[u]
+            ms = psum.tile([P, BANK], F32, name="ms", tag=f"back{u % 2}" if u in (THIRD, FOURTH) else "ms")
+            mx_pass(ms, wc_mx, b, src_w, src_s, h, True, True)
             za = psum.tile([P, BANK], F32, name="za", bufs=2)
-            mx_pass(za, wb_mx, 2 * P, b, src_w, src_s, h, True, False)
-            mx_pass(za, wa_mx, P, b, dst_w, dst_s, h, False, True)
+            mx_pass(za, wb_mx, b, src_w, src_s, h, True, False)
+            mx_pass(za, wa_mx, b, dst_w, dst_s, h, False, True)
             ow = psum.tile([P, BANK], F32, name="ow")
-            mx_pass(ow, wo_mx, P, b, dst_w, dst_s, h, True, True)
-            if b < 2 and h == 1:
-                eta = keep.tile([P, BANK], F32, name="held_eta", tag=("wo_grouped", "weighted1")[b], align_bytes=64)
-            else:
-                eta = ring.tile([P, BANK], F32, name="eta")
-            if (b, h) == (1, 1):
-                source = keep.tile([P, BANK], F32, name="held_source", tag=f"late_out{h}")
-            else:
-                source = ring.tile([P, BANK], F32, name="source")
-            if (b, h) == (0, 0):
-                message = keep.tile([P, BANK], F32, name="first_message", tag="wo_grouped", align_bytes=64)
-            elif (b, h) == (0, 1):
-                message = keep.tile([P, BANK], F32, name="third_message", tag="first_result")
-            else:
-                message = ring.tile([P, BANK], F32, name="message")
+            mx_pass(ow, wo_mx, b, dst_w, dst_s, h, True, True)
+            eta = stage_tile("eta", u, {THIRD: "wo_grouped", FOURTH: "weighted_second"}, True)
+            source = stage_tile("source", u, {FOURTH: "third_out"}, False)
+            message = stage_tile("message", u, {FIRST: "wo_grouped", THIRD: "first_result1"}, u == FIRST)
             nc.scalar.copy(out=source[:], in_=ms[:])
-            for part in parts(b, h):
-                cols = slice(part[0] * P, (part[-1] + 1) * P)
+            for part in parts(u):
+                cols = span(part)
                 nc.scalar.activation(eta[:, cols], za[:, cols], SIGMOID)
                 nc.gpsimd.tensor_tensor(message[:, cols], source[:, cols], eta[:, cols], MULT)
-            if (b, h) == (1, 1):
-                third = keep.tile([P, T], F32, name="late_out", tag=f"late_out{h}")
-                nc.gpsimd.memset(third[:].bitcast(I32), 0)
-                out_rows[2] = third
-            if (b, h) == (0, 1):
-                own = keep.tile([P, BANK], F32, name="held_own", tag="weighted0", align_bytes=64)
-            else:
-                own = ring.tile([P, BANK], F32, name="own")
-            for part in parts(b, h):
-                cols = slice(part[0] * P, (part[-1] + 1) * P)
-                nc.scalar.copy(out=own[:, cols], in_=ow[:, cols])
+            if u == FOURTH:
+                third_out = keep.tile([P, T], F32, name="third_out", tag="third_out")
+                nc.gpsimd.memset(third_out[:].bitcast(I32), 0)
+                out_rows.append(third_out)
+            own = stage_tile("own", u, {THIRD: "weighted_first"}, True)
+            for part in parts(u):
+                nc.scalar.copy(out=own[:, span(part)], in_=ow[:, span(part)])
             return message, own
 
-        def finish(b, h, message, own):
-            if (b, h) == (0, 0):
-                first_result = keep.tile([P, BANK], F32, name="first_result", tag="first_result")
-            terms = (own, picked[b][:, h * BANK : (h + 1) * BANK], message)
-            if b < 2 and h == 0:
-                weighted = keep.tile([P, BANK], F32, name="first_weighted", tag=f"weighted{b}", align_bytes=64)
-            else:
-                weighted = ring.tile([P, BANK], F32, name="weighted")
-            for part in parts(b, h):
+        def summed(u, message, own, targets):
+            b, h = UNITS[u]
+            weighted = stage_tile("weighted", u, {FIRST: "weighted_first", SECOND: "weighted_second"}, True)
+            for i, part in enumerate(parts(u)):
                 total = psum.tile([P, BANK], F32, name="total", bufs=2)
-                for i, term in enumerate(terms):
-                    for q in part:
-                        cols = slice(q * P, (q + 1) * P)
-                        nc.tensor.matmul(
-                            total[:, cols],
-                            term[:, cols],
-                            ident,
-                            start=(i == 0 and q == part[0]),
-                            stop=(i == len(terms) - 1 and q == part[-1]),
-                            is_transpose=True,
-                        )
-                for q in part:
-                    cols = slice(q * P, (q + 1) * P)
+                tiles = [slice(q * P, (q + 1) * P) for q in part]
+                terms = (
+                    [(cols, own[:, cols]) for cols in tiles]
+                    + [(cols, state(b, h * BANK + cols.start)) for cols in tiles]
+                    + [(cols, message[:, cols]) for cols in tiles]
+                )
+                for n, (cols, term) in enumerate(terms):
+                    nc.tensor.matmul(
+                        total[:, cols], term, ident[:], start=(n == 0), stop=(n == len(terms) - 1), is_transpose=True
+                    )
+                for q, cols in zip(part, tiles):
                     nc.scalar.activation(weighted[:, cols], total[:, cols], COPY, scale=wgo_cols[h][:, q : q + 1])
-                back = psum.tile([P, BANK], F32, name="back", tag=f"back{(units.index((b, h)) + part[0] // 2) % 2}")
-                for q in part:
-                    cols = slice(q * P, (q + 1) * P)
-                    nc.tensor.transpose(back[:, cols], weighted[:, cols], ident)
-                first, last = part[0] * P, (part[-1] + 1) * P
-                if (b, h) == (0, 0):
-                    nc.scalar.copy(out=first_result[:, first:last], in_=back[:, first:last])
-                else:
-                    nc.scalar.copy(out=result[b][:, h * BANK + first : h * BANK + last], in_=back[:, first:last])
-            cols = slice(h * BANK, (h + 1) * BANK)
+                back = psum.tile([P, BANK], F32, name="back", tag=f"back{(u + i) % 2}")
+                for cols in tiles:
+                    nc.tensor.transpose(back[:, cols], weighted[:, cols], ident[:])
+                nc.scalar.copy(out=targets[i], in_=back[:, span(part)])
+
+        def finish_first(message, own):
+            first_result = [keep.tile([P, PART], F32, name=f"first_result{i}", tag=f"first_result{i}") for i in range(2)]
+            summed(FIRST, message, own, [tile[:] for tile in first_result])
+            values = keep.tile([P, BANK], F32, name="first_values", tag="wgo_late", align_bytes=64)
+            nc.gpsimd.tensor_copy(values[:, 0:PART], first_result[0][:])
+            nc.vector.tensor_copy(first_out[:].indirect(entries(dst_list, 0, PART)), values[:, 0:PART])
+            tail = keep.tile([P, PART], F32, name="picked_tail", tag="first_result0")
+            nc.vector.tensor_copy(tail[:], r_rows[TAIL_SLAB][:].indirect(entries(dst_list, TAIL, J)))
+            picked_tail.append(tail)
+            nc.gpsimd.tensor_copy(values[:, PART:BANK], first_result[1][:])
+            nc.vector.tensor_copy(first_out[:].indirect(entries(dst_list, PART, BANK)), values[:, PART:BANK])
+
+        def finish(u, message, own):
+            b, h = UNITS[u]
+            first, last = h * BANK, (h + 1) * BANK
+            summed(u, message, own, [result[b][:, first:last]])
             window = out_rows[b % OUT_TILES][:]
-            if (b, h) == (0, 0):
-                values = keep.tile([P, BANK], F32, name="first_values", tag="wgo_late", align_bytes=64)
-                for first, last in ((0, FIRST_PART), (FIRST_PART, BANK)):
-                    nc.gpsimd.tensor_copy(values[:, first:last], first_result[:, first:last])
-                    nc.vector.tensor_copy(window.indirect(dst_list[:, first // 16 : last // 16]), values[:, first:last])
-            elif b < 2:
-                nc.vector.tensor_copy(window.indirect(half_list(dst_list, h)), result[b][:, cols])
+            if b < PAIRED:
+                nc.vector.tensor_copy(window.indirect(entries(dst_list, first, last)), result[b][:, first:last])
             elif h == HALVES - 1:
                 nc.vector.tensor_copy(window.indirect(dst_list[:]), result[b][:])
 
-        for first, last in ((0, FIRST_PART), (FIRST_PART, J)):
-            nc.vector.tensor_copy(picked[0][:, first:last], r_rows[0][:].indirect(dst_list[:, first // 16 : last // 16]))
-        for b in range(1, ROW_BLOCKS):
-            nc.vector.tensor_copy(picked[b][:], r_rows[b][:].indirect(dst_list[:]))
         def store(b):
-            rows = slice(b * P, (b + 1) * P)
-            tile = out_rows[b % OUT_TILES]
             width = T // STORE_PIECES[b]
             for i in range(STORE_PIECES[b]):
-                queue = nc.scalar if b == ROW_BLOCKS - 1 and i % 2 == 0 else nc.sync
-                queue.dma_start(out=out[rows, i * width : (i + 1) * width], in_=tile[:, i * width : (i + 1) * width])
+                cols = slice(i * width, (i + 1) * width)
+                queue = nc.scalar if b == SLABS - 1 and i % 2 == 0 else nc.sync
+                queue.dma_start(out=out[b * P : (b + 1) * P, cols], in_=out_rows[b % OUT_TILES][:, cols])
 
-
-        units = [(b, h) for h in range(HALVES) for b in range(2)] + [(b, h) for b in range(2, ROW_BLOCKS) for h in range(HALVES)]
-        staged = [unit(b, h) for b, h in units[:AHEAD]]
-        nc.gpsimd.tensor_copy(wgo_rows[1][0:TILES_PER_HALF, :], wgo_late[0:TILES_PER_HALF, :])
-
-        def turn_wgo(h, bank):
-            nc.tensor.transpose(bank[:, 0:P], wgo_rows[h], ident)
+        def turn_wgo(h):
+            bank = psum.tile([P, BANK], F32, name="wgo_bank", tag="ms")
+            nc.tensor.transpose(bank[:, 0:P], wgo_rows[h][:], ident[:])
             nc.scalar.copy(out=wgo_cols[h][:], in_=bank[:, 0:TILES_PER_HALF])
 
-        turn_wgo(0, psum.tile([P, BANK], F32, name="early_turn", tag="ms"))
-        for u, (b, h) in enumerate(units):
-            if (b, h) == (0, 1):
-                turn_wgo(1, psum.tile([P, BANK], F32, name="late_turn", tag="ms"))
-            finish(b, h, *staged[u])
+        staged = [products(u) for u in range(AHEAD)]
+        nc.gpsimd.tensor_copy(wgo_rows[1][0:TILES_PER_HALF, :], wgo_late[0:TILES_PER_HALF, :])
+        turn_wgo(0)
+        for u, (b, h) in enumerate(UNITS):
+            if u == THIRD:
+                turn_wgo(1)
+            if u == FIRST:
+                finish_first(*staged[u])
+            else:
+                finish(u, *staged[u])
             if h == HALVES - 1:
                 store(b)
-            if u + AHEAD < len(units):
-                staged.append(unit(*units[u + AHEAD]))
+            if u + AHEAD < len(UNITS):
+                staged.append(products(u + AHEAD))

@@ -22,39 +22,36 @@ P = 128
 PACK = 4
 BANK = 512
 PER_COLUMN = 16
+BLOCKS = K // 32
+QUADRANT = 32
 SLABS = N // P
 HALVES = J // BANK
 TILES_PER_HALF = BANK // P
-PAIRED = 2
-OUT_TILES = 3
+OUT_TILES = 2
+PART = 2 * P
+TAIL = J - PART
 AHEAD = 2
 STAGE_BUFS = 4
-PART = 2 * P
-TAIL_SLAB = 2
-TAIL = J - PART
-STORE_PIECES = (1, 2, 4, 4)
+STORE_PIECES = (2, 2, 2, 4)
 
-UNITS = [(b, h) for h in range(HALVES) for b in range(PAIRED)] + [
-    (b, h) for b in range(PAIRED, SLABS) for h in range(HALVES)
-]
-FIRST, SECOND, THIRD, FOURTH = range(4)
+UNITS = [(b, h) for b in range(SLABS) for h in range(HALVES)]
 
-
-def load_scale_quadrant(queue, plane, scales, q):
-    rows = scales[0].bitcast(I32)
-    queue.dma_start(out=plane[32 * q : 32 * q + 4, :], in_=rows[4 * q : 4 * q + 4, :])
+WA_RAW_AT = 0
+R_ROWS_AT = 4 * PACK * N
+WGO_AT = R_ROWS_AT + 4 * SLABS * T
+TAB_S_AT = WGO_AT - 512
+WGO_LATE_AT = WGO_AT + 512
+WO_GROUPED_AT = WGO_LATE_AT + 4 * BANK
+WA_GROUPED_AT = WO_GROUPED_AT + 2 * PACK * N
+PICKED_S_AT = WA_GROUPED_AT + 2 * PACK * N
+FOURTH_MESSAGE_AT = PICKED_S_AT + 2 * J
+FIRST_RESULT_AT = FOURTH_MESSAGE_AT + 4 * BANK - 512
+FIFTH_MESSAGE_AT = FOURTH_MESSAGE_AT + 4 * BANK
+TAIL_AT = WGO_LATE_AT
 
 
 def entries(lst, first, last):
     return lst[:, first // PER_COLUMN : last // PER_COLUMN]
-
-
-def parts(u):
-    return [(0, 1), (2, 3)] if u == FIRST else [(0, 1, 2, 3)]
-
-
-def span(part):
-    return slice(part[0] * P, (part[-1] + 1) * P)
 
 
 def tile_list_rgg_ownL_kernel(
@@ -63,104 +60,131 @@ def tile_list_rgg_ownL_kernel(
     nc = tc.nc
     with ExitStack() as ctx:
         keep = ctx.enter_context(tc.tile_pool(name="keep", bufs=1))
+        handed = ctx.enter_context(tc.tile_pool(name="handed", bufs=1))
         ring = ctx.enter_context(tc.tile_pool(name="ring", bufs=STAGE_BUFS))
         psum = ctx.enter_context(tc.psum_pool(name="psum", bufs=1))
+
+        def handed_tile(shape, dtype, name, at):
+            return handed.tile(shape, dtype, name=name, offset=at, align_bytes=64)
 
         src_list = keep.tile([P, J // PER_COLUMN], U16, name="src_list")
         dst_list = keep.tile([P, J // PER_COLUMN], U16, name="dst_list")
         tab_w = keep.tile([P, T], I32, name="tab_w", align_bytes=64)
-        tab_s = keep.tile([P, T // 4], I32, name="tab_s", tag="tab_s", align_bytes=64)
+        tab_s = handed_tile([P, T // 4], I32, "tab_s", TAB_S_AT)
         wb_w = keep.tile([P, N // 2], I32, name="wb_w", align_bytes=64)
-        wb_s = keep.tile([P, N // 4], I32, name="wb_s", align_bytes=64)
         wc_w = keep.tile([P, N], I32, name="wc_w", align_bytes=64)
-        wc_s = keep.tile([P, N // 4], I32, name="wc_s", align_bytes=64)
-        wa_raw = keep.tile([P, PACK, N], F32, name="wa_raw", tag="wa_raw", align_bytes=64)
+        w_planes = keep.tile([P, 2, N // 4], I32, name="w_planes", align_bytes=64)
+        wa_raw = handed_tile([P, PACK, N], F32, "wa_raw", WA_RAW_AT)
         wo_raw = keep.tile([P, PACK, N], F32, name="wo_raw")
-        wgo_cols = [keep.tile([P, TILES_PER_HALF], F32, name=f"wgo_cols{h}") for h in range(HALVES)]
-        r_rows = [keep.tile([P, T], F32, name=f"r_rows{b}") for b in range(SLABS)]
+        v_planes = keep.tile([P, 2 * J // 4], I32, name="v_planes", align_bytes=64)
         warm = keep.tile([P, 1], F32, name="warm")
         warmed = keep.tile([P, 1], F32, name="warmed")
-        wgo_rows = [keep.tile([P, P], F32, name=f"wgo_rows{h}", align_bytes=64) for h in range(HALVES)]
-        wgo_late = keep.tile([P, P], F32, name="wgo_late", tag="wgo_late", align_bytes=64)
         ident = keep.tile([P, P], F32, name="ident")
-        first_out = keep.tile([P, T], F32, name="first_out")
-        out_rows = [first_out]
+        wgo_cols = keep.tile([P, J // P], F32, name="wgo_cols")
 
-        nc.vector.memset(tab_s[:], 0)
-        nc.vector.memset(warm[:], 0.0)
-        nc.vector.memset(wc_s[:], 0)
-        for rows in wgo_rows:
-            nc.vector.memset(rows[:], 0.0)
-        nc.vector.memset(ident[:], 0.0)
-        make_identity(nc, ident[:], nomemset=True)
-        nc.vector.memset(wb_s[:], 0)
-        nc.vector.memset(first_out[:].bitcast(I32), 0)
-
-        for q in range(4):
-            load_scale_quadrant(nc.gpsimd, wb_s, wb_scales, q)
         nc.sync.dma_start(src_list[:], offs)
-        for q in (0, 2, 1, 3):
-            load_scale_quadrant(nc.sync, tab_s, tab_scales, q)
+        rows = tab_scales[0].bitcast(I32)
+        nc.scalar.dma_start(out=tab_s[0:QUADRANT, :], in_=rows.unsqueeze(1).to_broadcast([BLOCKS, 2, T // 4]))
+        nc.vector.memset(warm[:], 0.0)
+        nc.vector.memset(tab_s[QUADRANT : 2 * QUADRANT, :], 0)
+        nc.vector.memset(tab_s[2 * QUADRANT : P, :], 0)
+        nc.vector.memset(ident[:], 0.0)
+        nc.vector.memset(v_planes[:], 0)
         nc.scalar.activation(warmed[:], warm[:], SIGMOID)
+        make_identity(nc, ident[:], nomemset=True)
+
+        def load_weight_plane(queue, i, scales):
+            for q in range(4):
+                queue.dma_start(
+                    out=w_planes[QUADRANT * q : QUADRANT * (q + 1), i, :],
+                    in_=scales[0].bitcast(I32)[4 * q : 4 * q + 4, :].unsqueeze(0).to_broadcast([8, 4, N // 4]),
+                )
+
+        load_weight_plane(nc.gpsimd, 1, wb_scales)
+        out_rows = [keep.tile([P, T], F32, name=f"out_rows{i}") for i in range(OUT_TILES)]
+        for tile in out_rows:
+            nc.gpsimd.memset(tile[:].bitcast(I32), 0)
+
         nc.sync.dma_start(dst_list[:], offs2)
         nc.sync.dma_start(out=tab_w[:], in_=tab_words[0].rearrange("p t i -> p (t i)").bitcast(I32))
+        load_weight_plane(nc.sync, 0, wc_scales)
         nc.sync.dma_start(out=wa_raw[:], in_=wa.rearrange("(p i) n -> p i n", i=PACK))
-        for q in range(4):
-            load_scale_quadrant(nc.sync, wc_s, wc_scales, q)
         nc.sync.dma_start(out=wo_raw[:], in_=wo.rearrange("(p i) n -> p i n", i=PACK))
         nc.sync.dma_start(out=wc_w[:], in_=wc_words[0].rearrange("p n i -> p (n i)").bitcast(I32))
         nc.sync.dma_start(out=wb_w[:], in_=wb_words[0].bitcast(I32))
 
-        src_s = keep.tile([P, J], U8, name="src_s", align_bytes=64)
-        dst_s = keep.tile([P, J], U8, name="dst_s", align_bytes=64)
-        nc.vector.tensor_copy(src_s[:], tab_s[:].bitcast(U8).indirect(src_list[:]))
-        nc.vector.tensor_copy(dst_s[:], tab_s[:].bitcast(U8).indirect(dst_list[:]))
-        second_out = keep.tile([P, T], F32, name="second_out", tag="tab_s", align_bytes=64)
-        nc.gpsimd.memset(second_out[:].bitcast(I32), 0)
-        out_rows.append(second_out)
+        picked_s = handed_tile([P, 2 * J], U8, "picked_s", PICKED_S_AT)
+        nc.vector.tensor_copy(picked_s[:, 0:J], tab_s[:].bitcast(U8).indirect(src_list[:]))
+        nc.vector.tensor_copy(picked_s[:, J : 2 * J], tab_s[:].bitcast(U8).indirect(dst_list[:]))
 
-        for b in range(SLABS):
-            if b == 1:
-                nc.sync.dma_start(out=wgo_rows[0][0:TILES_PER_HALF, :], in_=wgo[0, 0:BANK].rearrange("(e p) -> e p", p=P))
-            if b == TAIL_SLAB + 1:
-                nc.sync.dma_start(out=wgo_late[0:TILES_PER_HALF, :], in_=wgo[0, BANK:J].rearrange("(e p) -> e p", p=P))
-            nc.sync.dma_start(out=r_rows[b][:], in_=rT[b * P : (b + 1) * P, :])
-
-        src_all = keep.tile([P, J], U32, name="src_all", align_bytes=64)
-        nc.vector.tensor_copy(src_all[:], tab_w[:].bitcast(U32).indirect(src_list[:]))
-        src_w = [src_all[:, h * BANK : (h + 1) * BANK] for h in range(HALVES)]
-        quantised, dst_w = [], []
-        for h, (label, raw) in enumerate((("wa", wa_raw), ("wo", wo_raw))):
-            dst_w.append(keep.tile([P, BANK], U32, name="dst_w", tag=("dst_first", "wa_raw")[h], align_bytes=64)[:])
-            nc.vector.tensor_copy(dst_w[h], tab_w[:].bitcast(U32).indirect(entries(dst_list, h * BANK, (h + 1) * BANK)))
-            grouped = keep.tile([P, N, PACK], BF16, name="grouped", tag=f"{label}_grouped", align_bytes=64)
-            codes = keep.tile([P, N], U32, name=f"{label}_codes", align_bytes=64)
-            plane = keep.tile([P, N], U8, name=f"{label}_plane", align_bytes=64)
+        def rounded(raw, name, at):
+            grouped = handed_tile([P, N, PACK], BF16, name, at)
             nc.scalar.copy(
                 out=grouped[:].rearrange("p (c n) i -> p c i n", n=PACK),
                 in_=raw[:].rearrange("p i (c n) -> p c i n", n=PACK),
             )
+            return grouped
+
+        def quantised(grouped, label):
+            codes = keep.tile([P, N], U32, name=f"{label}_codes", align_bytes=64)
+            plane = keep.tile([P, N], U8, name=f"{label}_plane", align_bytes=64)
             nc.vector.quantize_mx(
                 out=codes[:].bitcast(FP8X4), scales=plane[:], in_=grouped[:].rearrange("p n i -> p (n i)")
             )
-            quantised.append((codes[:], plane[:], FP8X4, P))
-        wa_mx, wo_mx = quantised
-        wb_mx = (wb_w[:].bitcast(U8), wb_s[:].bitcast(U8), FP4X4, 2 * P)
-        wc_mx = (wc_w[:], wc_s[:].bitcast(U8), FP8X4, P)
+            return codes[:], plane[:], FP8X4, P
+
+        def gathered_words(lst, h, label, at=None):
+            if at is None:
+                words = keep.tile([P, BANK], U32, name=f"{label}{h}", align_bytes=64)
+            else:
+                words = handed_tile([P, BANK], U32, f"{label}{h}", at)
+            nc.vector.tensor_copy(words[:], tab_w[:].bitcast(U32).indirect(entries(lst, h * BANK, (h + 1) * BANK)))
+            return words[:]
+
+        for q in range(4):
+            nc.sync.dma_start(
+                out=v_planes[QUADRANT * q : QUADRANT * q + 4, :], in_=picked_s[:].bitcast(I32)[8 * q : 8 * q + 8 : 2, :]
+            )
+        src_s = v_planes[:].bitcast(U8)[:, 0:J]
+        dst_s = v_planes[:].bitcast(U8)[:, J : 2 * J]
+        r_all = handed_tile([P, SLABS * T], F32, "r_all", R_ROWS_AT)
+        wgo_rows = handed_tile([P, P], F32, "wgo_rows", WGO_AT)
+        r_rows = [r_all[:, b * T : (b + 1) * T] for b in range(SLABS)]
+        for b in range(SLABS):
+            nc.sync.dma_start(out=r_rows[b], in_=rT[b * P : (b + 1) * P, :])
+            if b == 0:
+                nc.sync.dma_start(out=wgo_rows[:], in_=wgo[0 : P * P // J, :].rearrange("a (e p) -> (a e) p", p=P))
+        wgo_first = handed_tile([P, PART], F32, "wgo_first", WGO_LATE_AT)
+        nc.sync.dma_start(out=wgo_first[:], in_=wgo[:, 0:PART])
+
+        wa_grouped = rounded(wa_raw, "wa_grouped", WA_GROUPED_AT)
+        wo_grouped = rounded(wo_raw, "wo_grouped", WO_GROUPED_AT)
+        src_w = [gathered_words(src_list, 0, "src_w")]
+        dst_w = [gathered_words(dst_list, 0, "dst_w")]
+        src_w.append(gathered_words(src_list, 1, "src_w"))
+        wa_mx = quantised(wa_grouped, "wa")
+        dst_w.append(gathered_words(dst_list, 1, "dst_w", WA_RAW_AT))
+        wo_mx = quantised(wo_grouped, "wo")
+        wb_mx = (wb_w[:].bitcast(U8), w_planes[:, 1, :].bitcast(U8), FP4X4, 2 * P)
+        wc_mx = (wc_w[:], w_planes[:, 0, :].bitcast(U8), FP8X4, P)
 
         picked = [keep.tile([P, J], F32, name=f"picked{b}") for b in range(SLABS)]
         result = [keep.tile([P, J], F32, name=f"result{b}") for b in range(SLABS)]
-        for first, last in ((0, PART), (PART, J)):
-            nc.vector.tensor_copy(picked[0][:, first:last], r_rows[0][:].indirect(entries(dst_list, first, last)))
+        for first, last in ((0, BANK), (BANK, J)):
+            nc.vector.tensor_copy(picked[0][:, first:last], r_rows[0].indirect(entries(dst_list, first, last)))
         for b in range(1, SLABS):
-            last = TAIL if b == TAIL_SLAB else J
-            nc.vector.tensor_copy(picked[b][:, 0:last], r_rows[b][:].indirect(entries(dst_list, 0, last)))
+            last = TAIL if b == SLABS - 1 else J
+            nc.vector.tensor_copy(picked[b][:, 0:last], r_rows[b].indirect(entries(dst_list, 0, last)))
         picked_tail = []
 
         def state(b, edge):
-            if b == TAIL_SLAB and edge >= TAIL:
+            if b == SLABS - 1 and edge >= TAIL:
                 return picked_tail[0][:, edge - TAIL : edge - TAIL + P]
             return picked[b][:, edge : edge + P]
+
+        wgo_bank = psum.tile([P, BANK], F32, name="back", bufs=2)
+        nc.tensor.transpose(wgo_bank[:, 0:P], wgo_rows[:], ident[:])
+        nc.scalar.copy(out=wgo_cols[:], in_=wgo_bank[:, 0 : J // P])
 
         def mx_pass(bank, weight, b, words, plane, h, start, stop):
             w_words, w_plane, w_dtype, width = weight
@@ -174,82 +198,66 @@ def tile_list_rgg_ownL_kernel(
                 stop=stop,
             )
 
-        def stage_tile(name, u, takes_over, aligned):
-            if u not in takes_over:
-                return ring.tile([P, BANK], F32, name=name)
-            if aligned:
-                return keep.tile([P, BANK], F32, name=f"{name}{u}", tag=takes_over[u], align_bytes=64)
-            return keep.tile([P, BANK], F32, name=f"{name}{u}", tag=takes_over[u])
-
         def products(u):
             b, h = UNITS[u]
-            ms = psum.tile([P, BANK], F32, name="ms", tag=f"back{u % 2}" if u in (THIRD, FOURTH) else "ms")
+            ms = psum.tile([P, BANK], F32, name="ms")
             mx_pass(ms, wc_mx, b, src_w, src_s, h, True, True)
             za = psum.tile([P, BANK], F32, name="za", bufs=2)
             mx_pass(za, wb_mx, b, src_w, src_s, h, True, False)
             mx_pass(za, wa_mx, b, dst_w, dst_s, h, False, True)
             ow = psum.tile([P, BANK], F32, name="ow")
             mx_pass(ow, wo_mx, b, dst_w, dst_s, h, True, True)
-            eta = stage_tile("eta", u, {THIRD: "wo_grouped", FOURTH: "weighted_second"}, True)
-            source = stage_tile("source", u, {FOURTH: "third_out"}, False)
-            message = stage_tile("message", u, {FIRST: "wo_grouped", THIRD: "first_result1"}, u == FIRST)
+            eta = ring.tile([P, BANK], F32, name="eta", bufs=2)
+            source = ring.tile([P, BANK], F32, name="source")
+            if u == 0:
+                message = handed_tile([P, BANK], F32, "first_message", WO_GROUPED_AT)
+            elif u in (3, 4):
+                message = handed_tile([P, BANK], F32, f"message{u}", (FOURTH_MESSAGE_AT, FIFTH_MESSAGE_AT)[u - 3])
+            else:
+                message = ring.tile([P, BANK], F32, name="message")
             nc.scalar.copy(out=source[:], in_=ms[:])
-            for part in parts(u):
-                cols = span(part)
-                nc.scalar.activation(eta[:, cols], za[:, cols], SIGMOID)
-                nc.gpsimd.tensor_tensor(message[:, cols], source[:, cols], eta[:, cols], MULT)
-            if u == FOURTH:
-                third_out = keep.tile([P, T], F32, name="third_out", tag="third_out")
-                nc.gpsimd.memset(third_out[:].bitcast(I32), 0)
-                out_rows.append(third_out)
-            own = stage_tile("own", u, {THIRD: "weighted_first"}, True)
-            for part in parts(u):
-                nc.scalar.copy(out=own[:, span(part)], in_=ow[:, span(part)])
+            nc.scalar.activation(eta[:], za[:], SIGMOID)
+            nc.gpsimd.tensor_tensor(message[:], source[:], eta[:], MULT)
+            own = ring.tile([P, BANK], F32, name="own")
+            nc.scalar.copy(out=own[:], in_=ow[:])
             return message, own
-
-        def summed(u, message, own, targets):
-            b, h = UNITS[u]
-            weighted = stage_tile("weighted", u, {FIRST: "weighted_first", SECOND: "weighted_second"}, True)
-            for i, part in enumerate(parts(u)):
-                total = psum.tile([P, BANK], F32, name="total", bufs=2)
-                tiles = [slice(q * P, (q + 1) * P) for q in part]
-                terms = (
-                    [(cols, own[:, cols]) for cols in tiles]
-                    + [(cols, state(b, h * BANK + cols.start)) for cols in tiles]
-                    + [(cols, message[:, cols]) for cols in tiles]
-                )
-                for n, (cols, term) in enumerate(terms):
-                    nc.tensor.matmul(
-                        total[:, cols], term, ident[:], start=(n == 0), stop=(n == len(terms) - 1), is_transpose=True
-                    )
-                for q, cols in zip(part, tiles):
-                    nc.scalar.activation(weighted[:, cols], total[:, cols], COPY, scale=wgo_cols[h][:, q : q + 1])
-                back = psum.tile([P, BANK], F32, name="back", tag=f"back{(u + i) % 2}")
-                for cols in tiles:
-                    nc.tensor.transpose(back[:, cols], weighted[:, cols], ident[:])
-                nc.scalar.copy(out=targets[i], in_=back[:, span(part)])
-
-        def finish_first(message, own):
-            first_result = [keep.tile([P, PART], F32, name=f"first_result{i}", tag=f"first_result{i}") for i in range(2)]
-            summed(FIRST, message, own, [tile[:] for tile in first_result])
-            values = keep.tile([P, BANK], F32, name="first_values", tag="wgo_late", align_bytes=64)
-            nc.gpsimd.tensor_copy(values[:, 0:PART], first_result[0][:])
-            nc.vector.tensor_copy(first_out[:].indirect(entries(dst_list, 0, PART)), values[:, 0:PART])
-            tail = keep.tile([P, PART], F32, name="picked_tail", tag="first_result0")
-            nc.vector.tensor_copy(tail[:], r_rows[TAIL_SLAB][:].indirect(entries(dst_list, TAIL, J)))
-            picked_tail.append(tail)
-            nc.gpsimd.tensor_copy(values[:, PART:BANK], first_result[1][:])
-            nc.vector.tensor_copy(first_out[:].indirect(entries(dst_list, PART, BANK)), values[:, PART:BANK])
 
         def finish(u, message, own):
             b, h = UNITS[u]
             first, last = h * BANK, (h + 1) * BANK
-            summed(u, message, own, [result[b][:, first:last]])
+            weighted = ring.tile([P, BANK], F32, name="weighted")
+            total = psum.tile([P, BANK], F32, name="total", bufs=2)
+            tiles = [slice(q * P, (q + 1) * P) for q in range(TILES_PER_HALF)]
+            terms = (
+                [(cols, own[:, cols]) for cols in tiles]
+                + [(cols, state(b, first + cols.start)) for cols in tiles]
+                + [(cols, message[:, cols]) for cols in tiles]
+            )
+            for n, (cols, term) in enumerate(terms):
+                nc.tensor.matmul(
+                    total[:, cols], term, ident[:], start=(n == 0), stop=(n == len(terms) - 1), is_transpose=True
+                )
+            if u == 0:
+                nc.scalar.copy(out=weighted[:, 0:PART], in_=total[:, 0:PART])
+            for cols in tiles:
+                edge = first + cols.start
+                if u > 0 or edge >= PART:
+                    e = edge // P
+                    nc.scalar.activation(weighted[:, cols], total[:, cols], COPY, scale=wgo_cols[:, e : e + 1])
+            back = psum.tile([P, BANK], F32, name="back", bufs=2)
+            for cols in tiles:
+                nc.tensor.transpose(back[:, cols], weighted[:, cols], ident[:])
+            if u == 0:
+                unweighted = handed_tile([P, PART], F32, "unweighted", FIRST_RESULT_AT)
+                nc.scalar.copy(out=unweighted[:], in_=back[:, 0:PART])
+                nc.scalar.copy(out=result[0][:, PART:BANK], in_=back[:, PART:BANK])
+                nc.gpsimd.tensor_tensor(result[0][:, 0:PART], unweighted[:], wgo_first[:], MULT)
+            else:
+                nc.scalar.copy(out=result[b][:, first:last], in_=back[:])
+
+        def scatter(b, first, last):
             window = out_rows[b % OUT_TILES][:]
-            if b < PAIRED:
-                nc.vector.tensor_copy(window.indirect(entries(dst_list, first, last)), result[b][:, first:last])
-            elif h == HALVES - 1:
-                nc.vector.tensor_copy(window.indirect(dst_list[:]), result[b][:])
+            nc.vector.tensor_copy(window.indirect(entries(dst_list, first, last)), result[b][:, first:last])
 
         def store(b):
             width = T // STORE_PIECES[b]
@@ -258,22 +266,16 @@ def tile_list_rgg_ownL_kernel(
                 queue = nc.scalar if b == SLABS - 1 and i % 2 == 0 else nc.sync
                 queue.dma_start(out=out[b * P : (b + 1) * P, cols], in_=out_rows[b % OUT_TILES][:, cols])
 
-        def turn_wgo(h):
-            bank = psum.tile([P, BANK], F32, name="wgo_bank", tag="ms")
-            nc.tensor.transpose(bank[:, 0:P], wgo_rows[h][:], ident[:])
-            nc.scalar.copy(out=wgo_cols[h][:], in_=bank[:, 0:TILES_PER_HALF])
-
         staged = [products(u) for u in range(AHEAD)]
-        nc.gpsimd.tensor_copy(wgo_rows[1][0:TILES_PER_HALF, :], wgo_late[0:TILES_PER_HALF, :])
-        turn_wgo(0)
         for u, (b, h) in enumerate(UNITS):
-            if u == THIRD:
-                turn_wgo(1)
-            if u == FIRST:
-                finish_first(*staged[u])
-            else:
-                finish(u, *staged[u])
-            if h == HALVES - 1:
-                store(b)
+            finish(u, *staged[u])
             if u + AHEAD < len(UNITS):
                 staged.append(products(u + AHEAD))
+            if u == 0:
+                scatter(0, 0, PART)
+                tail = handed_tile([P, J - TAIL], F32, "picked_tail", TAIL_AT)
+                nc.vector.tensor_copy(tail[:], r_rows[SLABS - 1].indirect(entries(dst_list, TAIL, J)))
+                picked_tail.append(tail)
+            if h == HALVES - 1:
+                scatter(b, PART if b == 0 else 0, J)
+                store(b)

@@ -39,9 +39,10 @@ UNITS = [(b, h) for b in range(SLABS) for h in range(HALVES)]
 WA_RAW_AT = 0
 R_ROWS_AT = 4 * PACK * N
 WGO_AT = R_ROWS_AT + 4 * SLABS * T
-TAB_S_AT = WGO_AT - 512
+TAB_S_AT = WGO_AT - 256
 WGO_LATE_AT = WGO_AT + 512
-WO_GROUPED_AT = WGO_LATE_AT + 4 * BANK
+FIRST_OUT_AT = WGO_LATE_AT + 4 * PART
+WO_GROUPED_AT = FIRST_OUT_AT + 4 * T
 WA_GROUPED_AT = WO_GROUPED_AT + 2 * PACK * N
 PICKED_S_AT = WA_GROUPED_AT + 2 * PACK * N
 FOURTH_MESSAGE_AT = PICKED_S_AT + 2 * J
@@ -85,6 +86,7 @@ def tile_list_rgg_ownL_kernel(
         nc.sync.dma_start(src_list[:], offs)
         rows = tab_scales[0].bitcast(I32)
         nc.scalar.dma_start(out=tab_s[0:QUADRANT, :], in_=rows.unsqueeze(1).to_broadcast([BLOCKS, 2, T // 4]))
+        nc.vector.memset(w_planes[:], 0)
         nc.vector.memset(warm[:], 0.0)
         nc.vector.memset(tab_s[QUADRANT : 2 * QUADRANT, :], 0)
         nc.vector.memset(tab_s[2 * QUADRANT : P, :], 0)
@@ -96,14 +98,10 @@ def tile_list_rgg_ownL_kernel(
         def load_weight_plane(queue, i, scales):
             for q in range(4):
                 queue.dma_start(
-                    out=w_planes[QUADRANT * q : QUADRANT * (q + 1), i, :],
-                    in_=scales[0].bitcast(I32)[4 * q : 4 * q + 4, :].unsqueeze(0).to_broadcast([8, 4, N // 4]),
+                    out=w_planes[QUADRANT * q : QUADRANT * q + 4, i, :], in_=scales[0].bitcast(I32)[4 * q : 4 * q + 4, :]
                 )
 
         load_weight_plane(nc.gpsimd, 1, wb_scales)
-        out_rows = [keep.tile([P, T], F32, name=f"out_rows{i}") for i in range(OUT_TILES)]
-        for tile in out_rows:
-            nc.gpsimd.memset(tile[:].bitcast(I32), 0)
 
         nc.sync.dma_start(dst_list[:], offs2)
         nc.sync.dma_start(out=tab_w[:], in_=tab_words[0].rearrange("p t i -> p (t i)").bitcast(I32))
@@ -157,6 +155,10 @@ def tile_list_rgg_ownL_kernel(
         wgo_first = handed_tile([P, PART], F32, "wgo_first", WGO_LATE_AT)
         nc.sync.dma_start(out=wgo_first[:], in_=wgo[:, 0:PART])
 
+        first_out = handed_tile([P, T], F32, "first_out", FIRST_OUT_AT)
+        nc.gpsimd.memset(first_out[:].bitcast(I32), 0)
+        out_rows = [first_out]
+
         wa_grouped = rounded(wa_raw, "wa_grouped", WA_GROUPED_AT)
         wo_grouped = rounded(wo_raw, "wo_grouped", WO_GROUPED_AT)
         src_w = [gathered_words(src_list, 0, "src_w")]
@@ -208,7 +210,10 @@ def tile_list_rgg_ownL_kernel(
             ow = psum.tile([P, BANK], F32, name="ow")
             mx_pass(ow, wo_mx, b, dst_w, dst_s, h, True, True)
             eta = ring.tile([P, BANK], F32, name="eta", bufs=2)
-            source = ring.tile([P, BANK], F32, name="source")
+            if u == 3:
+                source = keep.tile([P, BANK], F32, name="source", tag="second_out")
+            else:
+                source = ring.tile([P, BANK], F32, name="source")
             if u == 0:
                 message = handed_tile([P, BANK], F32, "first_message", WO_GROUPED_AT)
             elif u in (3, 4):
@@ -218,6 +223,10 @@ def tile_list_rgg_ownL_kernel(
             nc.scalar.copy(out=source[:], in_=ms[:])
             nc.scalar.activation(eta[:], za[:], SIGMOID)
             nc.gpsimd.tensor_tensor(message[:], source[:], eta[:], MULT)
+            if u == 3:
+                second_out = keep.tile([P, T], F32, name="second_out", tag="second_out")
+                nc.gpsimd.memset(second_out[:].bitcast(I32), 0)
+                out_rows.append(second_out)
             own = ring.tile([P, BANK], F32, name="own")
             nc.scalar.copy(out=own[:], in_=ow[:])
             return message, own

@@ -40,11 +40,12 @@ WA_RAW_AT = 0
 R_ROWS_AT = 4 * PACK * N
 WGO_AT = R_ROWS_AT + 4 * SLABS * T
 TAB_S_AT = WGO_AT - 256
-WGO_LATE_AT = WGO_AT + 512
-FIRST_OUT_AT = WGO_LATE_AT + 4 * PART
+IDENT_AT = WGO_AT + 4 * P
+FIRST_OUT_AT = IDENT_AT + 4 * P
 WO_GROUPED_AT = FIRST_OUT_AT + 4 * T
 WA_GROUPED_AT = WO_GROUPED_AT + 2 * PACK * N
 PICKED_S_AT = WA_GROUPED_AT + 2 * PACK * N
+WGO_LATE_AT = PICKED_S_AT
 FOURTH_MESSAGE_AT = PICKED_S_AT + 2 * J
 FIRST_RESULT_AT = FOURTH_MESSAGE_AT + 4 * BANK - 512
 FIFTH_MESSAGE_AT = FOURTH_MESSAGE_AT + 4 * BANK
@@ -80,20 +81,18 @@ def tile_list_rgg_ownL_kernel(
         v_planes = keep.tile([P, 2 * J // 4], I32, name="v_planes", align_bytes=64)
         warm = keep.tile([P, 1], F32, name="warm")
         warmed = keep.tile([P, 1], F32, name="warmed")
-        ident = keep.tile([P, P], F32, name="ident")
         wgo_cols = keep.tile([P, J // P], F32, name="wgo_cols")
 
         nc.sync.dma_start(src_list[:], offs)
         rows = tab_scales[0].bitcast(I32)
         nc.scalar.dma_start(out=tab_s[0:QUADRANT, :], in_=rows.unsqueeze(1).to_broadcast([BLOCKS, 2, T // 4]))
-        nc.vector.memset(w_planes[:], 0)
+        nc.vector.memset(w_planes[:, 0, :], 0)
         nc.vector.memset(warm[:], 0.0)
         nc.vector.memset(tab_s[QUADRANT : 2 * QUADRANT, :], 0)
         nc.vector.memset(tab_s[2 * QUADRANT : P, :], 0)
-        nc.vector.memset(ident[:], 0.0)
         nc.vector.memset(v_planes[:], 0)
+        nc.vector.memset(w_planes[:, 1, :], 0)
         nc.scalar.activation(warmed[:], warm[:], SIGMOID)
-        make_identity(nc, ident[:], nomemset=True)
 
         def load_weight_plane(queue, i, scales):
             for q in range(4):
@@ -155,6 +154,8 @@ def tile_list_rgg_ownL_kernel(
         wgo_first = handed_tile([P, PART], F32, "wgo_first", WGO_LATE_AT)
         nc.sync.dma_start(out=wgo_first[:], in_=wgo[:, 0:PART])
 
+        ident = handed_tile([P, P], F32, "ident", IDENT_AT)
+        make_identity(nc, ident[:])
         first_out = handed_tile([P, T], F32, "first_out", FIRST_OUT_AT)
         nc.gpsimd.memset(first_out[:].bitcast(I32), 0)
         out_rows = [first_out]

@@ -83,9 +83,9 @@ def tile_list_rgg_ownL_kernel(
         warmed = keep.tile([P, 1], F32, name="warmed")
         wgo_cols = keep.tile([P, J // P], F32, name="wgo_cols")
 
-        nc.sync.dma_start(src_list[:], offs)
         rows = tab_scales[0].bitcast(I32)
-        nc.scalar.dma_start(out=tab_s[0:QUADRANT, :], in_=rows.unsqueeze(1).to_broadcast([BLOCKS, 2, T // 4]))
+        nc.sync.dma_start(out=tab_s[0:QUADRANT, :], in_=rows.unsqueeze(1).to_broadcast([BLOCKS, 2, T // 4]))
+        nc.sync.dma_start(src_list[:], offs)
         nc.vector.memset(w_planes[:, 0, :], 0)
         nc.vector.memset(warm[:], 0.0)
         nc.vector.memset(tab_s[QUADRANT : 2 * QUADRANT, :], 0)

@@ -32,7 +32,7 @@ PART = 2 * P
 TAIL = J - PART
 AHEAD = 2
 STAGE_BUFS = 4
-STORE_PIECES = (2, 2, 2, 4)
+STORE_PIECES = (2, 2, 4, 2)
 
 UNITS = [(b, h) for b in range(SLABS) for h in range(HALVES)]
 
@@ -273,8 +273,7 @@ def tile_list_rgg_ownL_kernel(
             width = T // STORE_PIECES[b]
             for i in range(STORE_PIECES[b]):
                 cols = slice(i * width, (i + 1) * width)
-                queue = nc.scalar if b == SLABS - 1 and i % 2 == 0 else nc.sync
-                queue.dma_start(out=out[b * P : (b + 1) * P, cols], in_=out_rows[b % OUT_TILES][:, cols])
+                nc.sync.dma_start(out=out[b * P : (b + 1) * P, cols], in_=out_rows[b % OUT_TILES][:, cols])
 
         staged = [products(u) for u in range(AHEAD)]
         for u, (b, h) in enumerate(UNITS):

@@ -29,10 +29,11 @@ HALVES = J // BANK
 TILES_PER_HALF = BANK // P
 OUT_TILES = 2
 PART = 2 * P
+WIDE = N // 2
 TAIL = J - PART
 AHEAD = 2
 STAGE_BUFS = 4
-STORE_PIECES = (2, 2, 4, 2)
+STORE_PIECES = (2, 2, 2, 2)
 
 UNITS = [(b, h) for b in range(SLABS) for h in range(HALVES)]
 
@@ -44,9 +45,9 @@ IDENT_AT = WGO_AT + 4 * P
 FIRST_OUT_AT = IDENT_AT + 4 * P
 WO_GROUPED_AT = FIRST_OUT_AT + 4 * T
 WA_GROUPED_AT = WO_GROUPED_AT + 2 * PACK * N
-PICKED_S_AT = WA_GROUPED_AT + 2 * PACK * N
-WGO_LATE_AT = PICKED_S_AT
-FOURTH_MESSAGE_AT = PICKED_S_AT + 2 * J
+PICKED_S_AT = WA_GROUPED_AT + 2 * PACK * N + 512
+WGO_LATE_AT = PICKED_S_AT + 64
+FOURTH_MESSAGE_AT = PICKED_S_AT + 2 * J + 64
 FIRST_RESULT_AT = FOURTH_MESSAGE_AT + 4 * BANK - 512
 FIFTH_MESSAGE_AT = FOURTH_MESSAGE_AT + 4 * BANK
 TAIL_AT = WGO_LATE_AT
@@ -73,8 +74,8 @@ def tile_list_rgg_ownL_kernel(
         dst_list = keep.tile([P, J // PER_COLUMN], U16, name="dst_list")
         tab_w = keep.tile([P, T], I32, name="tab_w", align_bytes=64)
         tab_s = handed_tile([P, T // 4], I32, "tab_s", TAB_S_AT)
-        wb_w = keep.tile([P, N // 2], I32, name="wb_w", align_bytes=64)
-        wc_w = keep.tile([P, N], I32, name="wc_w", align_bytes=64)
+        wb_w = [keep.tile([P, WIDE // 2], I32, name="wb_early", align_bytes=64)]
+        wc_w = [keep.tile([P, WIDE], I32, name="wc_early", align_bytes=64)]
         w_planes = keep.tile([P, 2, N // 4], I32, name="w_planes", align_bytes=64)
         wa_raw = handed_tile([P, PACK, N], F32, "wa_raw", WA_RAW_AT)
         wo_raw = keep.tile([P, PACK, N], F32, name="wo_raw")
@@ -107,8 +108,13 @@ def tile_list_rgg_ownL_kernel(
         load_weight_plane(nc.sync, 0, wc_scales)
         nc.sync.dma_start(out=wa_raw[:], in_=wa.rearrange("(p i) n -> p i n", i=PACK))
         nc.sync.dma_start(out=wo_raw[:], in_=wo.rearrange("(p i) n -> p i n", i=PACK))
-        nc.sync.dma_start(out=wc_w[:], in_=wc_words[0].rearrange("p n i -> p (n i)").bitcast(I32))
-        nc.sync.dma_start(out=wb_w[:], in_=wb_words[0].bitcast(I32))
+
+        def load_words(half):
+            wc_all = wc_words[0].rearrange("p n i -> p (n i)").bitcast(I32)
+            nc.sync.dma_start(out=wc_w[half][:], in_=wc_all[:, half * WIDE : (half + 1) * WIDE])
+            nc.sync.dma_start(out=wb_w[half][:], in_=wb_words[0].bitcast(I32)[:, half * WIDE // 2 : (half + 1) * WIDE // 2])
+
+        load_words(0)
 
         picked_s = handed_tile([P, 2 * J], U8, "picked_s", PICKED_S_AT)
         nc.vector.tensor_copy(picked_s[:, 0:J], tab_s[:].bitcast(U8).indirect(src_list[:]))
@@ -128,7 +134,7 @@ def tile_list_rgg_ownL_kernel(
             nc.vector.quantize_mx(
                 out=codes[:].bitcast(FP8X4), scales=plane[:], in_=grouped[:].rearrange("p n i -> p (n i)")
             )
-            return codes[:], plane[:], FP8X4, P
+            return [codes[:, 0:WIDE], codes[:, WIDE:N]], plane[:], FP8X4, P
 
         def gathered_words(lst, h, label, at=None):
             if at is None:
@@ -153,6 +159,9 @@ def tile_list_rgg_ownL_kernel(
                 nc.sync.dma_start(out=wgo_rows[:], in_=wgo[0 : P * P // J, :].rearrange("a (e p) -> (a e) p", p=P))
         wgo_first = handed_tile([P, PART], F32, "wgo_first", WGO_LATE_AT)
         nc.sync.dma_start(out=wgo_first[:], in_=wgo[:, 0:PART])
+        wc_w.append(handed_tile([P, WIDE], I32, "wc_late", WGO_LATE_AT + 4 * PART))
+        wb_w.append(handed_tile([P, WIDE // 2], I32, "wb_late", WGO_LATE_AT - 2 * WIDE))
+        load_words(1)
 
         ident = handed_tile([P, P], F32, "ident", IDENT_AT)
         make_identity(nc, ident[:])
@@ -168,8 +177,8 @@ def tile_list_rgg_ownL_kernel(
         wa_mx = quantised(wa_grouped, "wa")
         dst_w.append(gathered_words(dst_list, 1, "dst_w", WA_RAW_AT))
         wo_mx = quantised(wo_grouped, "wo")
-        wb_mx = (wb_w[:].bitcast(U8), w_planes[:, 1, :].bitcast(U8), FP4X4, 2 * P)
-        wc_mx = (wc_w[:], w_planes[:, 0, :].bitcast(U8), FP8X4, P)
+        wb_mx = ([w[:].bitcast(U8) for w in wb_w], w_planes[:, 1, :].bitcast(U8), FP4X4, 2 * P)
+        wc_mx = ([w[:] for w in wc_w], w_planes[:, 0, :].bitcast(U8), FP8X4, P)
 
         picked = [keep.tile([P, J], F32, name=f"picked{b}") for b in range(SLABS)]
         result = [keep.tile([P, J], F32, name=f"result{b}") for b in range(SLABS)]
@@ -193,7 +202,7 @@ def tile_list_rgg_ownL_kernel(
             w_words, w_plane, w_dtype, width = weight
             nc.tensor.matmul_mx(
                 out=bank[:],
-                lhsT=w_words[:, b * width : (b + 1) * width].bitcast(w_dtype),
+                lhsT=w_words[b // 2][:, b % 2 * width : (b % 2 + 1) * width].bitcast(w_dtype),
                 lhsT_scale=w_plane[:, b * P : (b + 1) * P],
                 rhs=words[h].bitcast(FP8X4),
                 rhs_scale=plane[:, h * BANK : (h + 1) * BANK],

@@ -24,6 +24,7 @@ BANK = 512
 PER_COLUMN = 16
 BLOCKS = K // 32
 QUADRANT = 32
+STAGED = P - BLOCKS
 SLABS = N // P
 HALVES = J // BANK
 TILES_PER_HALF = BANK // P
@@ -85,12 +86,11 @@ def tile_list_rgg_ownL_kernel(
         wgo_cols = keep.tile([P, J // P], F32, name="wgo_cols")
 
         rows = tab_scales[0].bitcast(I32)
-        nc.sync.dma_start(out=tab_s[0:QUADRANT, :], in_=rows.unsqueeze(1).to_broadcast([BLOCKS, 2, T // 4]))
+        nc.sync.dma_start(out=tab_s[STAGED:P, :], in_=rows)
         nc.sync.dma_start(src_list[:], offs)
         nc.vector.memset(w_planes[:, 0, :], 0)
         nc.vector.memset(warm[:], 0.0)
-        nc.vector.memset(tab_s[QUADRANT : 2 * QUADRANT, :], 0)
-        nc.vector.memset(tab_s[2 * QUADRANT : P, :], 0)
+        nc.vector.memset(tab_s[0:STAGED, :], 0)
         nc.vector.memset(v_planes[:], 0)
         nc.vector.memset(w_planes[:, 1, :], 0)
         nc.scalar.activation(warmed[:], warm[:], SIGMOID)
@@ -146,7 +146,7 @@ def tile_list_rgg_ownL_kernel(
 
         for q in range(4):
             nc.sync.dma_start(
-                out=v_planes[QUADRANT * q : QUADRANT * q + 4, :], in_=picked_s[:].bitcast(I32)[8 * q : 8 * q + 8 : 2, :]
+                out=v_planes[QUADRANT * q : QUADRANT * q + 4, :], in_=picked_s[:].bitcast(I32)[STAGED + 4 * q : STAGED + 4 * q + 4, :]
             )
         src_s = v_planes[:].bitcast(U8)[:, 0:J]
         dst_s = v_planes[:].bitcast(U8)[:, J : 2 * J]

from contextlib import ExitStack

import concourse.mybir as mybir
from concourse.masks import make_identity

K, N, T, J = 512, 512, 2048, 1024
FLOPS = 4 * 2 * K * N * J

F32 = mybir.dt.float32
BF16 = mybir.dt.bfloat16
I32 = mybir.dt.int32
U32 = mybir.dt.uint32
U16 = mybir.dt.uint16
U8 = mybir.dt.uint8
FP8X4 = mybir.dt.float8_e4m3fn_x4
FP4X4 = mybir.dt.float4_e2m1fn_x4
MULT = mybir.AluOpType.mult
COPY = mybir.ActivationFunctionType.Copy
SIGMOID = mybir.ActivationFunctionType.Sigmoid

P = 128
PACK = 4
BANK = 512
PER_COLUMN = 16
BLOCKS = K // 32
QUADRANT = 32
STAGED = P - BLOCKS
SLABS = N // P
HALVES = J // BANK
TILES_PER_HALF = BANK // P
OUT_TILES = 2
PART = 2 * P
WIDE = N // 2
TAIL = J - PART
AHEAD = 2
STAGE_BUFS = 4
STORE_PIECES = (2, 2, 2, 2)

UNITS = [(b, h) for b in range(SLABS) for h in range(HALVES)]

WA_RAW_AT = 0
R_ROWS_AT = 4 * PACK * N
WGO_AT = R_ROWS_AT + 4 * SLABS * T
TAB_S_AT = WGO_AT - 256
IDENT_AT = WGO_AT + 4 * P
FIRST_OUT_AT = IDENT_AT + 4 * P
WO_GROUPED_AT = FIRST_OUT_AT + 4 * T
WA_GROUPED_AT = WO_GROUPED_AT + 2 * PACK * N
PICKED_S_AT = WA_GROUPED_AT + 2 * PACK * N + 512
WGO_LATE_AT = PICKED_S_AT + 64
FOURTH_MESSAGE_AT = PICKED_S_AT + 2 * J + 64
FIRST_RESULT_AT = FOURTH_MESSAGE_AT + 4 * BANK - 512
FIFTH_MESSAGE_AT = FOURTH_MESSAGE_AT + 4 * BANK
TAIL_AT = WGO_LATE_AT


def entries(lst, first, last):
    return lst[:, first // PER_COLUMN : last // PER_COLUMN]


def tile_list_rgg_ownL_kernel(
    tc, tab_words, tab_scales, wa, wb_words, wb_scales, wc_words, wc_scales, wo, rT, wgo, offs, offs2, out
):
    nc = tc.nc
    with ExitStack() as ctx:
        keep = ctx.enter_context(tc.tile_pool(name="keep", bufs=1))
        handed = ctx.enter_context(tc.tile_pool(name="handed", bufs=1))
        ring = ctx.enter_context(tc.tile_pool(name="ring", bufs=STAGE_BUFS))
        psum = ctx.enter_context(tc.psum_pool(name="psum", bufs=1))

        def handed_tile(shape, dtype, name, at):
            return handed.tile(shape, dtype, name=name, offset=at, align_bytes=64)

        src_list = keep.tile([P, J // PER_COLUMN], U16, name="src_list")
        dst_list = keep.tile([P, J // PER_COLUMN], U16, name="dst_list")
        tab_w = keep.tile([P, T], I32, name="tab_w", align_bytes=64)
        tab_s = handed_tile([P, T // 4], I32, "tab_s", TAB_S_AT)
        wb_w = [keep.tile([P, WIDE // 2], I32, name="wb_early", align_bytes=64)]
        wc_w = [keep.tile([P, WIDE], I32, name="wc_early", align_bytes=64)]
        w_planes = keep.tile([P, 2, N // 4], I32, name="w_planes", align_bytes=64)
        wa_raw = handed_tile([P, PACK, N], F32, "wa_raw", WA_RAW_AT)
        wo_raw = keep.tile([P, PACK, N], F32, name="wo_raw")
        v_planes = keep.tile([P, 2 * J // 4], I32, name="v_planes", align_bytes=64)
        warm = keep.tile([P, 1], F32, name="warm")
        warmed = keep.tile([P, 1], F32, name="warmed")
        wgo_cols = keep.tile([P, J // P], F32, name="wgo_cols")

        rows = tab_scales[0].bitcast(I32)
        nc.sync.dma_start(out=tab_s[STAGED:P, :], in_=rows)
        nc.sync.dma_start(src_list[:], offs)
        nc.vector.memset(w_planes[:, 0, :], 0)
        nc.vector.memset(warm[:], 0.0)
        nc.vector.memset(tab_s[0:STAGED, :], 0)
        nc.vector.memset(v_planes[:], 0)
        nc.vector.memset(w_planes[:, 1, :], 0)
        nc.scalar.activation(warmed[:], warm[:], SIGMOID)

        def load_weight_plane(queue, i, scales):
            for q in range(4):
                queue.dma_start(
                    out=w_planes[QUADRANT * q : QUADRANT * q + 4, i, :], in_=scales[0].bitcast(I32)[4 * q : 4 * q + 4, :]
                )

        load_weight_plane(nc.gpsimd, 1, wb_scales)

        nc.sync.dma_start(dst_list[:], offs2)
        nc.sync.dma_start(out=tab_w[:], in_=tab_words[0].rearrange("p t i -> p (t i)").bitcast(I32))
        load_weight_plane(nc.sync, 0, wc_scales)
        nc.sync.dma_start(out=wa_raw[:], in_=wa.rearrange("(p i) n -> p i n", i=PACK))
        nc.sync.dma_start(out=wo_raw[:], in_=wo.rearrange("(p i) n -> p i n", i=PACK))

        def load_words(half):
            wc_all = wc_words[0].rearrange("p n i -> p (n i)").bitcast(I32)
            nc.sync.dma_start(out=wc_w[half][:], in_=wc_all[:, half * WIDE : (half + 1) * WIDE])
            nc.sync.dma_start(out=wb_w[half][:], in_=wb_words[0].bitcast(I32)[:, half * WIDE // 2 : (half + 1) * WIDE // 2])

        load_words(0)

        picked_s = handed_tile([P, 2 * J], U8, "picked_s", PICKED_S_AT)
        nc.vector.tensor_copy(picked_s[:, 0:J], tab_s[:].bitcast(U8).indirect(src_list[:]))
        nc.vector.tensor_copy(picked_s[:, J : 2 * J], tab_s[:].bitcast(U8).indirect(dst_list[:]))

        def rounded(raw, name, at):
            grouped = handed_tile([P, N, PACK], BF16, name, at)
            nc.scalar.copy(
                out=grouped[:].rearrange("p (c n) i -> p c i n", n=PACK),
                in_=raw[:].rearrange("p i (c n) -> p c i n", n=PACK),
            )
            return grouped

        def quantised(grouped, label):
            codes = keep.tile([P, N], U32, name=f"{label}_codes", align_bytes=64)
            plane = keep.tile([P, N], U8, name=f"{label}_plane", align_bytes=64)
            nc.vector.quantize_mx(
                out=codes[:].bitcast(FP8X4), scales=plane[:], in_=grouped[:].rearrange("p n i -> p (n i)")
            )
            return [codes[:, 0:WIDE], codes[:, WIDE:N]], plane[:], FP8X4, P

        def gathered_words(lst, h, label, at=None):
            if at is None:
                words = keep.tile([P, BANK], U32, name=f"{label}{h}", align_bytes=64)
            else:
                words = handed_tile([P, BANK], U32, f"{label}{h}", at)
            nc.vector.tensor_copy(words[:], tab_w[:].bitcast(U32).indirect(entries(lst, h * BANK, (h + 1) * BANK)))
            return words[:]

        for q in range(4):
            nc.sync.dma_start(
                out=v_planes[QUADRANT * q : QUADRANT * q + 4, :], in_=picked_s[:].bitcast(I32)[STAGED + 4 * q : STAGED + 4 * q + 4, :]
            )
        src_s = v_planes[:].bitcast(U8)[:, 0:J]
        dst_s = v_planes[:].bitcast(U8)[:, J : 2 * J]
        r_all = handed_tile([P, SLABS * T], F32, "r_all", R_ROWS_AT)
        wgo_rows = handed_tile([P, P], F32, "wgo_rows", WGO_AT)
        r_rows = [r_all[:, b * T : (b + 1) * T] for b in range(SLABS)]
        for b in range(SLABS):
            nc.sync.dma_start(out=r_rows[b], in_=rT[b * P : (b + 1) * P, :])
            if b == 0:
                nc.sync.dma_start(out=wgo_rows[:], in_=wgo[0 : P * P // J, :].rearrange("a (e p) -> (a e) p", p=P))
        wgo_first = handed_tile([P, PART], F32, "wgo_first", WGO_LATE_AT)
        nc.sync.dma_start(out=wgo_first[:], in_=wgo[:, 0:PART])
        wc_w.append(handed_tile([P, WIDE], I32, "wc_late", WGO_LATE_AT + 4 * PART))
        wb_w.append(handed_tile([P, WIDE // 2], I32, "wb_late", WGO_LATE_AT - 2 * WIDE))
        load_words(1)

        ident = handed_tile([P, P], F32, "ident", IDENT_AT)
        make_identity(nc, ident[:])
        first_out = handed_tile([P, T], F32, "first_out", FIRST_OUT_AT)
        nc.gpsimd.memset(first_out[:].bitcast(I32), 0)
        out_rows = [first_out]

        wa_grouped = rounded(wa_raw, "wa_grouped", WA_GROUPED_AT)
        wo_grouped = rounded(wo_raw, "wo_grouped", WO_GROUPED_AT)
        src_w = [gathered_words(src_list, 0, "src_w")]
        dst_w = [gathered_words(dst_list, 0, "dst_w")]
        src_w.append(gathered_words(src_list, 1, "src_w"))
        wa_mx = quantised(wa_grouped, "wa")
        dst_w.append(gathered_words(dst_list, 1, "dst_w", WA_RAW_AT))
        wo_mx = quantised(wo_grouped, "wo")
        wb_mx = ([w[:].bitcast(U8) for w in wb_w], w_planes[:, 1, :].bitcast(U8), FP4X4, 2 * P)
        wc_mx = ([w[:] for w in wc_w], w_planes[:, 0, :].bitcast(U8), FP8X4, P)

        picked = [keep.tile([P, J], F32, name=f"picked{b}") for b in range(SLABS)]
        result = [keep.tile([P, J], F32, name=f"result{b}") for b in range(SLABS)]
        for first, last in ((0, BANK), (BANK, J)):
            nc.vector.tensor_copy(picked[0][:, first:last], r_rows[0].indirect(entries(dst_list, first, last)))
        for b in range(1, SLABS):
            last = TAIL if b == SLABS - 1 else J
            nc.vector.tensor_copy(picked[b][:, 0:last], r_rows[b].indirect(entries(dst_list, 0, last)))
        picked_tail = []

        def state(b, edge):
            if b == SLABS - 1 and edge >= TAIL:
                return picked_tail[0][:, edge - TAIL : edge - TAIL + P]
            return picked[b][:, edge : edge + P]

        wgo_bank = psum.tile([P, BANK], F32, name="back", bufs=2)
        nc.tensor.transpose(wgo_bank[:, 0:P], wgo_rows[:], ident[:])
        nc.scalar.copy(out=wgo_cols[:], in_=wgo_bank[:, 0 : J // P])

        def mx_pass(bank, weight, b, words, plane, h, start, stop):
            w_words, w_plane, w_dtype, width = weight
            nc.tensor.matmul_mx(
                out=bank[:],
                lhsT=w_words[b // 2][:, b % 2 * width : (b % 2 + 1) * width].bitcast(w_dtype),
                lhsT_scale=w_plane[:, b * P : (b + 1) * P],
                rhs=words[h].bitcast(FP8X4),
                rhs_scale=plane[:, h * BANK : (h + 1) * BANK],
                start=start,
                stop=stop,
            )

        def products(u):
            b, h = UNITS[u]
            ms = psum.tile([P, BANK], F32, name="ms")
            mx_pass(ms, wc_mx, b, src_w, src_s, h, True, True)
            za = psum.tile([P, BANK], F32, name="za", bufs=2)
            mx_pass(za, wb_mx, b, src_w, src_s, h, True, False)
            mx_pass(za, wa_mx, b, dst_w, dst_s, h, False, True)
            ow = psum.tile([P, BANK], F32, name="ow")
            mx_pass(ow, wo_mx, b, dst_w, dst_s, h, True, True)
            eta = ring.tile([P, BANK], F32, name="eta", bufs=2)
            if u == 3:
                source = keep.tile([P, BANK], F32, name="source", tag="second_out")
            else:
                source = ring.tile([P, BANK], F32, name="source")
            if u == 0:
                message = handed_tile([P, BANK], F32, "first_message", WO_GROUPED_AT)
            elif u in (3, 4):
                message = handed_tile([P, BANK], F32, f"message{u}", (FOURTH_MESSAGE_AT, FIFTH_MESSAGE_AT)[u - 3])
            else:
                message = ring.tile([P, BANK], F32, name="message")
            nc.scalar.copy(out=source[:], in_=ms[:])
            nc.scalar.activation(eta[:], za[:], SIGMOID)
            nc.gpsimd.tensor_tensor(message[:], source[:], eta[:], MULT)
            if u == 3:
                second_out = keep.tile([P, T], F32, name="second_out", tag="second_out")
                nc.gpsimd.memset(second_out[:].bitcast(I32), 0)
                out_rows.append(second_out)
            own = ring.tile([P, BANK], F32, name="own")
            nc.scalar.copy(out=own[:], in_=ow[:])
            return message, own

        def finish(u, message, own):
            b, h = UNITS[u]
            first, last = h * BANK, (h + 1) * BANK
            weighted = ring.tile([P, BANK], F32, name="weighted")
            total = psum.tile([P, BANK], F32, name="total", bufs=2)
            tiles = [slice(q * P, (q + 1) * P) for q in range(TILES_PER_HALF)]
            terms = (
                [(cols, own[:, cols]) for cols in tiles]
                + [(cols, state(b, first + cols.start)) for cols in tiles]
                + [(cols, message[:, cols]) for cols in tiles]
            )
            for n, (cols, term) in enumerate(terms):
                nc.tensor.matmul(
                    total[:, cols], term, ident[:], start=(n == 0), stop=(n == len(terms) - 1), is_transpose=True
                )
            if u == 0:
                nc.scalar.copy(out=weighted[:, 0:PART], in_=total[:, 0:PART])
            for cols in tiles:
                edge = first + cols.start
                if u > 0 or edge >= PART:
                    e = edge // P
                    nc.scalar.activation(weighted[:, cols], total[:, cols], COPY, scale=wgo_cols[:, e : e + 1])
            back = psum.tile([P, BANK], F32, name="back", bufs=2)
            for cols in tiles:
                nc.tensor.transpose(back[:, cols], weighted[:, cols], ident[:])
            if u == 0:
                unweighted = handed_tile([P, PART], F32, "unweighted", FIRST_RESULT_AT)
                nc.scalar.copy(out=unweighted[:], in_=back[:, 0:PART])
                nc.scalar.copy(out=result[0][:, PART:BANK], in_=back[:, PART:BANK])
                nc.gpsimd.tensor_tensor(result[0][:, 0:PART], unweighted[:], wgo_first[:], MULT)
            else:
                nc.scalar.copy(out=result[b][:, first:last], in_=back[:])

        def scatter(b, first, last):
            window = out_rows[b % OUT_TILES][:]
            nc.vector.tensor_copy(window.indirect(entries(dst_list, first, last)), result[b][:, first:last])

        def store(b):
            width = T // STORE_PIECES[b]
            for i in range(STORE_PIECES[b]):
                cols = slice(i * width, (i + 1) * width)
                nc.sync.dma_start(out=out[b * P : (b + 1) * P, cols], in_=out_rows[b % OUT_TILES][:, cols])

        staged = [products(u) for u in range(AHEAD)]
        for u, (b, h) in enumerate(UNITS):
            finish(u, *staged[u])
            if u + AHEAD < len(UNITS):
                staged.append(products(u + AHEAD))
            if u == 0:
                scatter(0, 0, PART)
                tail = handed_tile([P, J - TAIL], F32, "picked_tail", TAIL_AT)
                nc.vector.tensor_copy(tail[:], r_rows[SLABS - 1].indirect(entries(dst_list, TAIL, J)))
                picked_tail.append(tail)
            if h == HALVES - 1:
                scatter(b, PART if b == 0 else 0, J)
                store(b)
